import numpy as np
import ml_dtypes


def mxq(x, axis, fmt="e4m3"):
    dtype, down = {"e4m3": (ml_dtypes.float8_e4m3fn, 7), "e5m2": (ml_dtypes.float8_e5m2, 14)}[fmt]
    v = np.moveaxis(np.asarray(x, np.float32).astype(ml_dtypes.bfloat16).astype(np.float64), axis, -1)
    blocks = v.reshape(v.shape[:-1] + (-1, 32))
    amax = np.abs(blocks).max(-1, keepdims=True)
    byte = np.maximum(np.where(amax > 0, np.frexp(amax)[1] - 1 + 127, 0) - down, 1)
    scale = np.exp2(byte - 127.0)
    codes = (blocks / scale).astype(np.float32).astype(dtype).astype(np.float64)
    return np.moveaxis((codes * scale).reshape(v.shape), -1, axis)


WIDE = False


def mx_kscale(k):
    if not WIDE:
        return np.ones(k)
    levels = np.array([10, -10, 5, -5, 0])
    if k % 512:
        return np.exp2(np.random.permutation(np.resize(levels, k // 32))).repeat(32)
    a = np.empty((k // 512, 16))
    for p in range(k // 512):
        a[p, :8] = np.random.permutation(np.resize(levels, 8))
        for g in range(8):
            far = levels[np.abs(levels - a[p, g]) >= 10]
            a[p, g + 8] = far[np.random.randint(len(far))]
    return np.exp2(a.ravel()).repeat(32)


def f64(x):
    return np.asarray(x).astype(np.float64)


def striped(idx):
    return np.tile(idx.reshape(-1, 16).T, (8, 1)).astype(np.uint16)


def unstriped(offs):
    return offs[:16].T.reshape(-1).astype(np.int64)


def pack_weight(w):
    k, n = w.shape
    w = f64(np.asarray(w, np.float32).astype(ml_dtypes.bfloat16)).reshape(k // 32, 32, n)
    amax = np.abs(w).max(1)
    byte = np.clip(np.where(amax > 0, np.frexp(amax)[1] - 1 + 127 - 7, 1), 1, 254)
    scaled = (w * np.exp2(127.0 - byte)[:, None, :]).reshape(k, n).astype(np.float32)
    words = np.ascontiguousarray(scaled.reshape(k // 512, 128, 4, n).transpose(0, 1, 3, 2)).astype(ml_dtypes.float8_e4m3fn).view(np.uint8)
    return words, np.ascontiguousarray(byte.astype(np.uint8).reshape(k // 512, 16, n))


def unpack_weight(words, scales):
    g, p, n, _ = words.shape
    vals = np.ascontiguousarray(words).view(ml_dtypes.float8_e4m3fn).astype(np.float64) * np.repeat(np.exp2(scales.astype(np.float64) - 127.0), 8, axis=1)[..., None]
    return vals.transpose(0, 1, 3, 2).reshape(g * 512, n)


def relu(v):
    return np.maximum(v, 0.0)


K, T, S, H, N = 512, 4096, 1024, 512, 256


def setup_inputs():
    n = np.random.standard_normal
    s = mx_kscale(K)[:, None]
    u = mx_kscale(H)
    packed_xT = pack_weight(n((K, T)) * s)
    return {
        "x_words": packed_xT[0],
        "x_scales": packed_xT[1],
        "w1": (n((K, H)) / np.sqrt(K) / s).astype(np.float32),
        "w2": (n((H, N)) / np.sqrt(H) / u[:, None]).astype(np.float32),
        "gamma": (np.random.uniform(0.5, 1.5, (H, 1)) * u[:, None]).astype(np.float32),
        "offs": striped(np.random.permutation(T)[:S]),
    }


def reference(x_words, x_scales, w1, w2, gamma, offs):
    xq = unpack_weight(x_words, x_scales)[:, unstriped(offs)]
    h = mxq(f64(w1), 0, "e4m3").T @ xq
    hn = (h - h.mean(axis=1, keepdims=True)) / np.sqrt(h.var(axis=1, keepdims=True) + 1e-5)
    z = relu(f64(gamma) * hn)
    return mxq(f64(w2), 0, "e4m3").T @ mxq(z, 0, "e4m3")

@@ -1,0 +1,226 @@
+from contextlib import ExitStack
+
+import concourse.mybir as mybir
+
+K, T, S, H, N = 512, 4096, 1024, 512, 256
+FLOPS = 2 * K * H * S + 2 * H * N * S
+EPS = 1e-5
+
+F32 = mybir.dt.float32
+BF16 = mybir.dt.bfloat16
+I32 = mybir.dt.int32
+U32 = mybir.dt.uint32
+U16 = mybir.dt.uint16
+U8 = mybir.dt.uint8
+FP8X4 = mybir.dt.float8_e4m3fn_x4
+ALU = mybir.AluOpType
+ACT = mybir.ActivationFunctionType
+
+P = 128
+PACK = 4
+HALF = 512
+QUARTER = 256
+
+
+def tile_picked_inorm_relu_p_kernel(tc, x_words, x_scales, w1, w2, gamma, offs, out):
+    nc = tc.nc
+    with ExitStack() as ctx:
+        keep = ctx.enter_context(tc.tile_pool(name="keep", bufs=1))
+        psum = ctx.enter_context(tc.psum_pool(name="psum", bufs=1))
+
+        offsets = keep.tile([P, S // 16], U16, name="offsets")
+        table_words = keep.tile([P, T], U32, name="table_words", align_bytes=64)
+        table_scales = keep.tile([P, T], U8, name="table_scales", align_bytes=64)
+        w1_raw = keep.tile([P, PACK, H], F32, name="w1_raw")
+        w2_raw = keep.tile([P, PACK, N], F32, name="w2_raw")
+        gamma_sb = keep.tile([P, PACK], F32, name="gamma_sb")
+
+        nc.vector.memset(table_scales[:].bitcast(I32), 0)
+        nc.sync.dma_start(out=w1_raw[:], in_=w1.rearrange("(p j) c -> p j c", j=PACK))
+        for q in range(4):
+            nc.sync.dma_start(
+                out=table_scales[32 * q : 32 * q + 4, :].bitcast(I32),
+                in_=x_scales[0, 4 * q : 4 * q + 4, :].bitcast(I32),
+            )
+        nc.sync.dma_start(offsets[:], offs)
+        nc.sync.dma_start(
+            out=table_words[:].bitcast(I32),
+            in_=x_words[0].rearrange("p n t -> p (n t)").bitcast(I32),
+        )
+        nc.sync.dma_start(out=w2_raw[:], in_=w2.rearrange("(p j) c -> p j c", j=PACK))
+        nc.sync.dma_start(out=gamma_sb[:], in_=gamma.rearrange("(p t) o -> p (t o)", t=PACK))
+
+        warm_in = keep.tile([P, 1], F32, name="warm_in")
+        warm_out = keep.tile([P, 1], F32, name="warm_out")
+        nc.gpsimd.memset(warm_in[:], 1.0)
+        nc.scalar.activation(out=warm_out[:], in_=warm_in[:], func=ACT.Abs_reciprocal_sqrt)
+
+        stats = [keep.tile([P, 15], F32, name=f"stats{t}") for t in range(PACK)]
+        moments = [keep.tile([P, 4], F32, name=f"moments{t}") for t in range(PACK)]
+        for t in range(PACK):
+            nc.vector.memset(moments[t][:, 0:1], -float(HALF))
+            nc.vector.memset(moments[t][:, 1:2], -1.0)
+        for t in (1, 2):
+            nc.vector.memset(stats[t][:, 0:1], float(HALF))
+
+        w1_bf = keep.tile([P, H * PACK], BF16, name="w1_bf", align_bytes=64)
+        nc.scalar.copy(
+            out=w1_bf[:].rearrange("p (t m j) -> p m t j", t=PACK, j=PACK),
+            in_=w1_raw[:].rearrange("p j (m t) -> p m t j", t=PACK),
+        )
+        x_sc = keep.tile([P, S], U8, name="x_sc", align_bytes=64)
+        nc.vector.tensor_copy(x_sc[:], table_scales[:].indirect(offsets[:]))
+        w1_codes = keep.tile([P, H], U32, name="w1_codes", align_bytes=64)
+        w1_sc = keep.tile([P, H], U8, name="w1_sc", align_bytes=64)
+        nc.vector.quantize_mx(out=w1_codes[:].bitcast(FP8X4), scales=w1_sc[:], in_=w1_bf[:])
+
+        x_codes = [keep.tile([P, HALF], U32, name=f"x_codes{u}", align_bytes=64) for u in range(2)]
+        for u in range(2):
+            nc.vector.tensor_copy(x_codes[u][:], table_words[:].indirect(offsets[:, 32 * u : 32 * (u + 1)]))
+
+        w2_bf = keep.tile([P, N, PACK], BF16, name="w2_bf", align_bytes=64)
+        nc.scalar.copy(out=w2_bf[:], in_=w2_raw[:].rearrange("p j n -> p n j"))
+
+        h = {}
+        for t, u in [(0, 0), (1, 0), (0, 1), (2, 0), (1, 1), (2, 1), (3, 0), (3, 1)]:
+            bank = psum.tile([P, HALF], F32, name=f"h{t}{u}", tag=f"bank{2 * t + u}")
+            nc.tensor.matmul_mx(
+                out=bank[:],
+                lhsT=w1_codes[:, P * t : P * (t + 1)].bitcast(FP8X4),
+                lhsT_scale=w1_sc[:, P * t : P * (t + 1)],
+                rhs=x_codes[u][:].bitcast(FP8X4),
+                rhs_scale=x_sc[:, HALF * u : HALF * (u + 1)],
+                start=True,
+                stop=True,
+            )
+            h[t, u] = bank
+
+        z_rows = [keep.tile([P, PACK, HALF], BF16, name=f"z_rows{u}", align_bytes=64) for u in range(2)]
+        affine = [keep.tile([P, 3], F32, name=f"affine{t}") for t in range(PACK)]
+        shrunk = {}
+
+        def stats_vector(t, u):
+            lo = 3 + 6 * u if t in (0, 3) else 3
+            nc.vector.bn_stats(out=stats[t][:, lo : lo + 6], in_=h[t, u][:])
+
+        def stats_scalar(t):
+            part = keep.tile([P, HALF], F32, name=f"shrunk{t}")
+            nc.scalar.activation(
+                out=part[:], in_=h[t, 0][:], func=ACT.Copy, scale=1.0 / HALF, accum_out=stats[t][:, 1:2]
+            )
+            squares = keep.tile([P, HALF], BF16, name=f"squares{t}")
+            nc.scalar.activation(
+                out=squares[:], in_=h[t, 0][:], func=ACT.Square, scale=-1.0, bias=stats[t][:, 1:2],
+                accum_out=stats[t][:, 2:3],
+            )
+            shrunk[t] = part
+
+        def aggregate(t):
+            tuples = stats[t][:, 3:15] if t in (0, 3) else stats[t][:, 0:9]
+            nc.vector.bn_aggr(out=moments[t][:, 2:4], in_=tuples)
+            factors = keep.tile([P, 3], F32, name=f"factors{t}")
+            nc.vector.tensor_scalar(
+                out=factors[:], in0=moments[t][:, 0:3], scalar1=gamma_sb[:, t : t + 1], scalar2=-1.0,
+                op0=ALU.mult, op1=ALU.mult,
+            )
+            rstd = keep.tile([P, 1], F32, name=f"rstd{t}")
+            nc.scalar.activation(out=rstd[:], in_=moments[t][:, 3:4], func=ACT.Abs_reciprocal_sqrt, bias=EPS)
+            nc.scalar.activation(out=affine[t][:], in_=factors[:], func=ACT.Copy, scale=rstd[:])
+
+        def normalise_scalar(t, u):
+            nc.scalar.activation(
+                out=z_rows[u][:, t, :], in_=h[t, u][:], func=ACT.Relu,
+                scale=affine[t][:, 1:2], bias=affine[t][:, 2:3],
+            )
+
+        def normalise_vector(t):
+            source, col = (shrunk[t], 0) if t in shrunk else (h[t, 0], 1)
+            nc.vector.tensor_scalar(
+                out=z_rows[0][:, t, :], in0=source[:], scalar1=affine[t][:, col : col + 1], scalar2=affine[t][:, 2:3],
+                op0=ALU.mult, op1=ALU.add,
+            )
+
+        stats_vector(0, 0)
+        stats_scalar(1)
+        stats_vector(0, 1)
+        aggregate(0)
+        stats_vector(1, 1)
+        aggregate(1)
+        stats_scalar(2)
+        stats_vector(2, 1)
+        aggregate(2)
+        stats_vector(3, 0)
+        stats_vector(3, 1)
+        aggregate(3)
+        normalise_scalar(0, 0)
+        normalise_vector(1)
+        normalise_vector(2)
+        normalise_vector(3)
+        for t in range(PACK):
+            normalise_scalar(t, 1)
+
+        w2_codes = keep.tile([P, N], U32, name="w2_codes", align_bytes=64)
+        w2_sc = keep.tile([P, N], U8, name="w2_sc", align_bytes=64)
+        nc.vector.quantize_mx(out=w2_codes[:].bitcast(FP8X4), scales=w2_sc[:], in_=w2_bf[:].rearrange("p n j -> p (n j)"))
+
+        z_bf = [keep.tile([P, QUARTER * PACK], BF16, name=f"z_bf{c}", align_bytes=64) for c in range(4)]
+        z_codes = [keep.tile([P, QUARTER], U32, name=f"z_codes{c}", align_bytes=64) for c in range(4)]
+        z_sc = [keep.tile([P, QUARTER], U8, name=f"z_sc{c}", align_bytes=64) for c in range(4)]
+
+        def rows_of(c):
+            u, v = divmod(c, 2)
+            return z_rows[u][:, :, QUARTER * v : QUARTER * (v + 1)].rearrange("p t (g i) -> p g t i", i=4)
+
+        def words_of(c):
+            return z_bf[c][:].rearrange("p (g i t) -> p g t i", i=4, t=PACK)
+
+        def interleave_vector(c):
+            nc.vector.tensor_scalar_max(out=words_of(c), in0=rows_of(c), scalar1=0.0)
+
+        def interleave_scalar(c):
+            nc.scalar.copy(out=words_of(c), in_=rows_of(c))
+
+        def quantise(c):
+            nc.vector.quantize_mx(out=z_codes[c][:].bitcast(FP8X4), scales=z_sc[c][:], in_=z_bf[c][:])
+
+        def product(c, m, acc):
+            nc.tensor.matmul_mx(
+                out=acc,
+                lhsT=w2_codes[:, P * m : P * (m + 1)].bitcast(FP8X4),
+                lhsT_scale=w2_sc[:, P * m : P * (m + 1)],
+                rhs=z_codes[c][:].bitcast(FP8X4),
+                rhs_scale=z_sc[c][:],
+                start=True,
+                stop=True,
+            )
+
+        def second_layer(c):
+            acc = psum.tile([P, 2, QUARTER], F32, name=f"acc{c}", tag=f"bank{2 * c}")
+            for m in range(2):
+                product(c, m, acc[:, m, :])
+            res = keep.tile([P, 2, QUARTER], F32, name=f"res{c}")
+            nc.scalar.copy(out=res[:], in_=acc[:])
+            nc.sync.dma_start(
+                out=out[:, QUARTER * c : QUARTER * (c + 1)].rearrange("(m p) n -> p m n", p=P), in_=res[:]
+            )
+
+        def last_second_layer(c):
+            for m, engine_copy in enumerate((nc.scalar.copy, nc.vector.tensor_copy)):
+                acc = psum.tile([P, QUARTER], F32, name=f"acc{c}{m}", tag=f"bank{2 * m + 1}")
+                product(c, m, acc[:])
+                res = keep.tile([P, QUARTER], F32, name=f"res{c}{m}")
+                engine_copy(out=res[:], in_=acc[:])
+                nc.sync.dma_start(out=out[P * m : P * (m + 1), QUARTER * c : QUARTER * (c + 1)], in_=res[:])
+
+        interleave_vector(0)
+        interleave_vector(1)
+        quantise(0)
+        quantise(1)
+        interleave_scalar(3)
+        second_layer(0)
+        second_layer(1)
+        interleave_vector(2)
+        quantise(3)
+        quantise(2)
+        second_layer(3)
+        last_second_layer(2)

@@ -36,13 +36,11 @@ def tile_picked_inorm_relu_p_kernel(tc, x_words, x_scales, w1, w2, gamma, offs, 
         gamma_sb = keep.tile([P, PACK], F32, name="gamma_sb")
 
         nc.vector.memset(table_scales[:].bitcast(I32), 0)
-        nc.sync.dma_start(out=w1_raw[:], in_=w1.rearrange("(p j) c -> p j c", j=PACK))
-        for q in range(4):
-            nc.sync.dma_start(
-                out=table_scales[32 * q : 32 * q + 4, :].bitcast(I32),
-                in_=x_scales[0, 4 * q : 4 * q + 4, :].bitcast(I32),
-            )
+        w1_rows = w1.rearrange("(p j) c -> p j c", j=PACK)
         nc.sync.dma_start(offsets[:], offs)
+        nc.sync.dma_start(out=w1_raw[:, :2, :], in_=w1_rows[:, :2, :])
+        nc.sync.dma_start(out=table_scales[0:P:8, :].bitcast(I32), in_=x_scales[0].bitcast(I32))
+        nc.sync.dma_start(out=w1_raw[:, 2:, :], in_=w1_rows[:, 2:, :])
         nc.sync.dma_start(
             out=table_words[:].bitcast(I32),
             in_=x_words[0].rearrange("p n t -> p (n t)").bitcast(I32),
@@ -68,8 +66,14 @@ def tile_picked_inorm_relu_p_kernel(tc, x_words, x_scales, w1, w2, gamma, offs, 
             out=w1_bf[:].rearrange("p (t m j) -> p m t j", t=PACK, j=PACK),
             in_=w1_raw[:].rearrange("p j (m t) -> p m t j", t=PACK),
         )
+        picked_sc = keep.tile([P, S], U8, name="picked_sc", align_bytes=64)
+        nc.vector.tensor_copy(picked_sc[:], table_scales[:].indirect(offsets[:]))
         x_sc = keep.tile([P, S], U8, name="x_sc", align_bytes=64)
-        nc.vector.tensor_copy(x_sc[:], table_scales[:].indirect(offsets[:]))
+        nc.vector.memset(x_sc[:].bitcast(I32), 0)
+        for q in range(4):
+            nc.scalar.dma_start(
+                out=x_sc[32 * q : 32 * q + 4, :].bitcast(I32), in_=picked_sc[32 * q : 32 * (q + 1) : 8, :].bitcast(I32)
+            )
         w1_codes = keep.tile([P, H], U32, name="w1_codes", align_bytes=64)
         w1_sc = keep.tile([P, H], U8, name="w1_sc", align_bytes=64)
         nc.vector.quantize_mx(out=w1_codes[:].bitcast(FP8X4), scales=w1_sc[:], in_=w1_bf[:])
@@ -95,6 +99,9 @@ def tile_picked_inorm_relu_p_kernel(tc, x_words, x_scales, w1, w2, gamma, offs, 
             )
             h[t, u] = bank
 
+        neg_gamma = keep.tile([P, PACK], F32, name="neg_gamma")
+        nc.scalar.activation(out=neg_gamma[:], in_=gamma_sb[:], func=ACT.Copy, scale=-1.0)
+
         z_rows = [keep.tile([P, PACK, HALF], BF16, name=f"z_rows{u}", align_bytes=64) for u in range(2)]
         affine = [keep.tile([P, 3], F32, name=f"affine{t}") for t in range(PACK)]
         shrunk = {}
@@ -118,14 +125,12 @@ def tile_picked_inorm_relu_p_kernel(tc, x_words, x_scales, w1, w2, gamma, offs, 
         def aggregate(t):
             tuples = stats[t][:, 3:15] if t in (0, 3) else stats[t][:, 0:9]
             nc.vector.bn_aggr(out=moments[t][:, 2:4], in_=tuples)
-            factors = keep.tile([P, 3], F32, name=f"factors{t}")
-            nc.vector.tensor_scalar(
-                out=factors[:], in0=moments[t][:, 0:3], scalar1=gamma_sb[:, t : t + 1], scalar2=-1.0,
-                op0=ALU.mult, op1=ALU.mult,
-            )
             rstd = keep.tile([P, 1], F32, name=f"rstd{t}")
             nc.scalar.activation(out=rstd[:], in_=moments[t][:, 3:4], func=ACT.Abs_reciprocal_sqrt, bias=EPS)
-            nc.scalar.activation(out=affine[t][:], in_=factors[:], func=ACT.Copy, scale=rstd[:])
+            nc.vector.tensor_scalar(
+                out=affine[t][:], in0=moments[t][:, 0:3], scalar1=neg_gamma[:, t : t + 1], scalar2=rstd[:],
+                op0=ALU.mult, op1=ALU.mult,
+            )
 
         def normalise_scalar(t, u):
             nc.scalar.activation(
@@ -195,7 +200,7 @@ def tile_picked_inorm_relu_p_kernel(tc, x_words, x_scales, w1, w2, gamma, offs, 
             )
 
         def second_layer(c):
-            acc = psum.tile([P, 2, QUARTER], F32, name=f"acc{c}", tag=f"bank{2 * c}")
+            acc = psum.tile([P, 2, QUARTER], F32, name=f"acc{c}", tag=f"bank{(2, 4, 0, 0)[c]}")
             for m in range(2):
                 product(c, m, acc[:, m, :])
             res = keep.tile([P, 2, QUARTER], F32, name=f"res{c}")

@@ -58,7 +58,7 @@ def tile_picked_inorm_relu_p_kernel(tc, x_words, x_scales, w1, w2, gamma, offs, 
         for t in range(PACK):
             nc.vector.memset(moments[t][:, 0:1], -float(HALF))
             nc.vector.memset(moments[t][:, 1:2], -1.0)
-        for t in (1, 2):
+        for t in (0, 2):
             nc.vector.memset(stats[t][:, 0:1], float(HALF))
 
         w1_bf = keep.tile([P, H * PACK], BF16, name="w1_bf", align_bytes=64)
@@ -82,8 +82,6 @@ def tile_picked_inorm_relu_p_kernel(tc, x_words, x_scales, w1, w2, gamma, offs, 
         for u in range(2):
             nc.vector.tensor_copy(x_codes[u][:], table_words[:].indirect(offsets[:, 32 * u : 32 * (u + 1)]))
 
-        w2_bf = keep.tile([P, N, PACK], BF16, name="w2_bf", align_bytes=64)
-        nc.scalar.copy(out=w2_bf[:], in_=w2_raw[:].rearrange("p j n -> p n j"))
 
         h = {}
         for t, u in [(0, 0), (1, 0), (0, 1), (2, 0), (1, 1), (2, 1), (3, 0), (3, 1)]:
@@ -102,12 +100,12 @@ def tile_picked_inorm_relu_p_kernel(tc, x_words, x_scales, w1, w2, gamma, offs, 
         neg_gamma = keep.tile([P, PACK], F32, name="neg_gamma")
         nc.scalar.activation(out=neg_gamma[:], in_=gamma_sb[:], func=ACT.Copy, scale=-1.0)
 
-        z_rows = [keep.tile([P, PACK, HALF], BF16, name=f"z_rows{u}", align_bytes=64) for u in range(2)]
+        z_rows = [keep.tile([P, PACK, QUARTER], BF16, name=f"z_rows{c}", align_bytes=64) for c in range(4)]
         affine = [keep.tile([P, 3], F32, name=f"affine{t}") for t in range(PACK)]
         shrunk = {}
 
         def stats_vector(t, u):
-            lo = 3 + 6 * u if t in (0, 3) else 3
+            lo = 3 + 6 * u if t in (1, 3) else 3
             nc.vector.bn_stats(out=stats[t][:, lo : lo + 6], in_=h[t, u][:])
 
         def stats_scalar(t):
@@ -115,7 +113,7 @@ def tile_picked_inorm_relu_p_kernel(tc, x_words, x_scales, w1, w2, gamma, offs, 
             nc.scalar.activation(
                 out=part[:], in_=h[t, 0][:], func=ACT.Copy, scale=1.0 / HALF, accum_out=stats[t][:, 1:2]
             )
-            squares = keep.tile([P, HALF], BF16, name=f"squares{t}")
+            squares = keep.tile([P, HALF], BF16, name=f"squares{t}", tag=f"scratch{t}", align_bytes=64)
             nc.scalar.activation(
                 out=squares[:], in_=h[t, 0][:], func=ACT.Square, scale=-1.0, bias=stats[t][:, 1:2],
                 accum_out=stats[t][:, 2:3],
@@ -123,30 +121,34 @@ def tile_picked_inorm_relu_p_kernel(tc, x_words, x_scales, w1, w2, gamma, offs, 
             shrunk[t] = part
 
         def aggregate(t):
-            tuples = stats[t][:, 3:15] if t in (0, 3) else stats[t][:, 0:9]
+            tuples = stats[t][:, 3:15] if t in (1, 3) else stats[t][:, 0:9]
             nc.vector.bn_aggr(out=moments[t][:, 2:4], in_=tuples)
             rstd = keep.tile([P, 1], F32, name=f"rstd{t}")
             nc.scalar.activation(out=rstd[:], in_=moments[t][:, 3:4], func=ACT.Abs_reciprocal_sqrt, bias=EPS)
-            nc.vector.tensor_scalar(
+            engine = nc.gpsimd if t == 0 else nc.vector
+            engine.tensor_scalar(
                 out=affine[t][:], in0=moments[t][:, 0:3], scalar1=neg_gamma[:, t : t + 1], scalar2=rstd[:],
                 op0=ALU.mult, op1=ALU.mult,
             )
 
-        def normalise_scalar(t, u):
+        def quarter_of(half_tile, c):
+            return half_tile[:, QUARTER * (c % 2) : QUARTER * (c % 2 + 1)]
+
+        def normalise_scalar(t, c):
             nc.scalar.activation(
-                out=z_rows[u][:, t, :], in_=h[t, u][:], func=ACT.Relu,
+                out=z_rows[c][:, t, :], in_=quarter_of(h[t, c // 2], c), func=ACT.Relu,
                 scale=affine[t][:, 1:2], bias=affine[t][:, 2:3],
             )
 
-        def normalise_vector(t):
+        def normalise_vector(t, c):
             source, col = (shrunk[t], 0) if t in shrunk else (h[t, 0], 1)
             nc.vector.tensor_scalar(
-                out=z_rows[0][:, t, :], in0=source[:], scalar1=affine[t][:, col : col + 1], scalar2=affine[t][:, 2:3],
-                op0=ALU.mult, op1=ALU.add,
+                out=z_rows[c][:, t, :], in0=quarter_of(source, c), scalar1=affine[t][:, col : col + 1],
+                scalar2=affine[t][:, 2:3], op0=ALU.mult, op1=ALU.add,
             )
 
-        stats_vector(0, 0)
-        stats_scalar(1)
+        stats_scalar(0)
+        stats_vector(1, 0)
         stats_vector(0, 1)
         aggregate(0)
         stats_vector(1, 1)
@@ -157,12 +159,23 @@ def tile_picked_inorm_relu_p_kernel(tc, x_words, x_scales, w1, w2, gamma, offs, 
         stats_vector(3, 0)
         stats_vector(3, 1)
         aggregate(3)
-        normalise_scalar(0, 0)
-        normalise_vector(1)
-        normalise_vector(2)
-        normalise_vector(3)
-        for t in range(PACK):
+        w2_bf = keep.tile([P, N, PACK], BF16, name="w2_bf", tag="scratch0", align_bytes=64)
+        w2_cols = w2_raw[:].rearrange("p j n -> p n j")
+        for n0 in range(0, N, 64):
+            nc.gpsimd.tensor_scalar(
+                out=w2_bf[:, n0 : n0 + 64, :], in0=w2_cols[:, n0 : n0 + 64, :],
+                scalar1=1.0, scalar2=0.0, op0=ALU.mult, op1=ALU.add,
+            )
+        normalise_scalar(1, 0)
+        normalise_vector(0, 0)
+        normalise_vector(2, 0)
+        normalise_vector(3, 0)
+        for t in (1, 2, 3):
             normalise_scalar(t, 1)
+        normalise_vector(0, 1)
+        for c in (3, 2):
+            for t in range(PACK):
+                normalise_scalar(t, c)
 
         w2_codes = keep.tile([P, N], U32, name="w2_codes", align_bytes=64)
         w2_sc = keep.tile([P, N], U8, name="w2_sc", align_bytes=64)
@@ -173,17 +186,16 @@ def tile_picked_inorm_relu_p_kernel(tc, x_words, x_scales, w1, w2, gamma, offs, 
         z_sc = [keep.tile([P, QUARTER], U8, name=f"z_sc{c}", align_bytes=64) for c in range(4)]
 
         def rows_of(c):
-            u, v = divmod(c, 2)
-            return z_rows[u][:, :, QUARTER * v : QUARTER * (v + 1)].rearrange("p t (g i) -> p g t i", i=4)
+            return z_rows[c][:].rearrange("p t (g i) -> p g t i", i=4)
 
         def words_of(c):
             return z_bf[c][:].rearrange("p (g i t) -> p g t i", i=4, t=PACK)
 
-        def interleave_vector(c):
-            nc.vector.tensor_scalar_max(out=words_of(c), in0=rows_of(c), scalar1=0.0)
+        def interleave_vector(c, groups=slice(0, QUARTER // 4)):
+            nc.vector.tensor_scalar_max(out=words_of(c)[:, groups], in0=rows_of(c)[:, groups], scalar1=0.0)
 
-        def interleave_scalar(c):
-            nc.scalar.copy(out=words_of(c), in_=rows_of(c))
+        def interleave_scalar(c, groups):
+            nc.scalar.copy(out=words_of(c)[:, groups], in_=rows_of(c)[:, groups])
 
         def quantise(c):
             nc.vector.quantize_mx(out=z_codes[c][:].bitcast(FP8X4), scales=z_sc[c][:], in_=z_bf[c][:])
@@ -200,7 +212,7 @@ def tile_picked_inorm_relu_p_kernel(tc, x_words, x_scales, w1, w2, gamma, offs, 
             )
 
         def second_layer(c):
-            acc = psum.tile([P, 2, QUARTER], F32, name=f"acc{c}", tag=f"bank{(2, 4, 0, 0)[c]}")
+            acc = psum.tile([P, 2, QUARTER], F32, name=f"acc{c}", tag=f"bank{(0, 4, 2, 2)[c]}")
             for m in range(2):
                 product(c, m, acc[:, m, :])
             res = keep.tile([P, 2, QUARTER], F32, name=f"res{c}")
@@ -221,9 +233,10 @@ def tile_picked_inorm_relu_p_kernel(tc, x_words, x_scales, w1, w2, gamma, offs, 
         interleave_vector(1)
         quantise(0)
         quantise(1)
-        interleave_scalar(3)
+        interleave_scalar(3, slice(0, QUARTER // 8))
         second_layer(0)
         second_layer(1)
+        interleave_vector(3, slice(QUARTER // 8, QUARTER // 4))
         interleave_vector(2)
         quantise(3)
         quantise(2)

@@ -20,6 +20,7 @@ P = 128
 PACK = 4
 HALF = 512
 QUARTER = 256
+W1_SPLIT = 88
 
 
 def tile_picked_inorm_relu_p_kernel(tc, x_words, x_scales, w1, w2, gamma, offs, out):
@@ -62,10 +63,9 @@ def tile_picked_inorm_relu_p_kernel(tc, x_words, x_scales, w1, w2, gamma, offs, 
             nc.vector.memset(stats[t][:, 0:1], float(HALF))
 
         w1_bf = keep.tile([P, H * PACK], BF16, name="w1_bf", align_bytes=64)
-        nc.scalar.copy(
-            out=w1_bf[:].rearrange("p (t m j) -> p m t j", t=PACK, j=PACK),
-            in_=w1_raw[:].rearrange("p j (m t) -> p m t j", t=PACK),
-        )
+        w1_dealt = w1_bf[:].rearrange("p (t m j) -> p m t j", t=PACK, j=PACK)
+        w1_cols = w1_raw[:].rearrange("p j (m t) -> p m t j", t=PACK)
+        nc.scalar.copy(out=w1_dealt[:, W1_SPLIT:], in_=w1_cols[:, W1_SPLIT:])
         picked_sc = keep.tile([P, S], U8, name="picked_sc", align_bytes=64)
         nc.vector.tensor_copy(picked_sc[:], table_scales[:].indirect(offsets[:]))
         x_sc = keep.tile([P, S], U8, name="x_sc", align_bytes=64)
@@ -74,6 +74,7 @@ def tile_picked_inorm_relu_p_kernel(tc, x_words, x_scales, w1, w2, gamma, offs, 
             nc.scalar.dma_start(
                 out=x_sc[32 * q : 32 * q + 4, :].bitcast(I32), in_=picked_sc[32 * q : 32 * (q + 1) : 8, :].bitcast(I32)
             )
+        nc.vector.tensor_copy(out=w1_dealt[:, :W1_SPLIT], in_=w1_cols[:, :W1_SPLIT])
         w1_codes = keep.tile([P, H], U32, name="w1_codes", align_bytes=64)
         w1_sc = keep.tile([P, H], U8, name="w1_sc", align_bytes=64)
         nc.vector.quantize_mx(out=w1_codes[:].bitcast(FP8X4), scales=w1_sc[:], in_=w1_bf[:])
@@ -82,6 +83,18 @@ def tile_picked_inorm_relu_p_kernel(tc, x_words, x_scales, w1, w2, gamma, offs, 
         for u in range(2):
             nc.vector.tensor_copy(x_codes[u][:], table_words[:].indirect(offsets[:, 32 * u : 32 * (u + 1)]))
 
+
+        warm_bank = psum.tile([P, HALF], F32, name="warm_bank", tag="bank7")
+        for i in range(3):
+            nc.tensor.matmul_mx(
+                out=warm_bank[:],
+                lhsT=w1_codes[:, 0:P].bitcast(FP8X4),
+                lhsT_scale=w1_sc[:, 0:P],
+                rhs=w1_codes[:].bitcast(FP8X4),
+                rhs_scale=w1_sc[:],
+                start=True,
+                stop=True,
+            )
 
         h = {}
         for t, u in [(0, 0), (1, 0), (0, 1), (2, 0), (1, 1), (2, 1), (3, 0), (3, 1)]:

@@ -20,7 +20,8 @@ P = 128
 PACK = 4
 HALF = 512
 QUARTER = 256
-W1_SPLIT = 88
+FIRST_COLS = 1024
+SCALAR_STATS = (0, 1)
 
 
 def tile_picked_inorm_relu_p_kernel(tc, x_words, x_scales, w1, w2, gamma, offs, out):
@@ -37,15 +38,12 @@ def tile_picked_inorm_relu_p_kernel(tc, x_words, x_scales, w1, w2, gamma, offs, 
         gamma_sb = keep.tile([P, PACK], F32, name="gamma_sb")
 
         nc.vector.memset(table_scales[:].bitcast(I32), 0)
-        w1_rows = w1.rearrange("(p j) c -> p j c", j=PACK)
+        words = x_words[0].rearrange("p n t -> p (n t)").bitcast(I32)
+        nc.sync.dma_start(out=table_words[:, :FIRST_COLS].bitcast(I32), in_=words[:, :FIRST_COLS])
         nc.sync.dma_start(offsets[:], offs)
-        nc.sync.dma_start(out=w1_raw[:, :2, :], in_=w1_rows[:, :2, :])
         nc.sync.dma_start(out=table_scales[0:P:8, :].bitcast(I32), in_=x_scales[0].bitcast(I32))
-        nc.sync.dma_start(out=w1_raw[:, 2:, :], in_=w1_rows[:, 2:, :])
-        nc.sync.dma_start(
-            out=table_words[:].bitcast(I32),
-            in_=x_words[0].rearrange("p n t -> p (n t)").bitcast(I32),
-        )
+        nc.sync.dma_start(out=table_words[:, FIRST_COLS:].bitcast(I32), in_=words[:, FIRST_COLS:])
+        nc.sync.dma_start(out=w1_raw[:], in_=w1.rearrange("(p j) c -> p j c", j=PACK))
         nc.sync.dma_start(out=w2_raw[:], in_=w2.rearrange("(p j) c -> p j c", j=PACK))
         nc.sync.dma_start(out=gamma_sb[:], in_=gamma.rearrange("(p t) o -> p (t o)", t=PACK))
 
@@ -57,47 +55,54 @@ def tile_picked_inorm_relu_p_kernel(tc, x_words, x_scales, w1, w2, gamma, offs, 
         stats = [keep.tile([P, 15], F32, name=f"stats{t}") for t in range(PACK)]
         moments = [keep.tile([P, 4], F32, name=f"moments{t}") for t in range(PACK)]
         for t in range(PACK):
-            nc.vector.memset(moments[t][:, 0:1], -float(HALF))
+            if t in SCALAR_STATS:
+                nc.vector.memset(moments[t][:, 0:1], -float(HALF))
+                nc.vector.memset(stats[t][:, 0:1], float(HALF))
             nc.vector.memset(moments[t][:, 1:2], -1.0)
-        for t in (0, 2):
-            nc.vector.memset(stats[t][:, 0:1], float(HALF))
 
-        w1_bf = keep.tile([P, H * PACK], BF16, name="w1_bf", align_bytes=64)
-        w1_dealt = w1_bf[:].rearrange("p (t m j) -> p m t j", t=PACK, j=PACK)
-        w1_cols = w1_raw[:].rearrange("p j (m t) -> p m t j", t=PACK)
-        nc.scalar.copy(out=w1_dealt[:, W1_SPLIT:], in_=w1_cols[:, W1_SPLIT:])
         picked_sc = keep.tile([P, S], U8, name="picked_sc", align_bytes=64)
         nc.vector.tensor_copy(picked_sc[:], table_scales[:].indirect(offsets[:]))
         x_sc = keep.tile([P, S], U8, name="x_sc", align_bytes=64)
-        nc.vector.memset(x_sc[:].bitcast(I32), 0)
-        for q in range(4):
-            nc.scalar.dma_start(
-                out=x_sc[32 * q : 32 * q + 4, :].bitcast(I32), in_=picked_sc[32 * q : 32 * (q + 1) : 8, :].bitcast(I32)
-            )
-        nc.vector.tensor_copy(out=w1_dealt[:, :W1_SPLIT], in_=w1_cols[:, :W1_SPLIT])
-        w1_codes = keep.tile([P, H], U32, name="w1_codes", align_bytes=64)
-        w1_sc = keep.tile([P, H], U8, name="w1_sc", align_bytes=64)
-        nc.vector.quantize_mx(out=w1_codes[:].bitcast(FP8X4), scales=w1_sc[:], in_=w1_bf[:])
+        nc.vector.tensor_copy(x_sc[:].bitcast(I32), picked_sc[:].bitcast(I32))
+        for r in range(1, 4):
+            nc.scalar.dma_start(out=x_sc[r:P:32, :].bitcast(I32), in_=picked_sc[8 * r : P : 32, :].bitcast(I32))
 
         x_codes = [keep.tile([P, HALF], U32, name=f"x_codes{u}", align_bytes=64) for u in range(2)]
         for u in range(2):
             nc.vector.tensor_copy(x_codes[u][:], table_words[:].indirect(offsets[:, 32 * u : 32 * (u + 1)]))
 
+        w1_bf = [keep.tile([P, 2, P * PACK], BF16, name=f"w1_bf{e}", align_bytes=64) for e in range(2)]
+        w1_cols = w1_raw[:].rearrange("p j (m t) -> p m j t", t=PACK)
+        for e, engine_copy in enumerate((nc.vector.tensor_copy, nc.scalar.copy)):
+            engine_copy(
+                out=w1_bf[e][:].rearrange("p t (m j) -> p m j t", j=PACK), in_=w1_cols[:, :, :, 2 * e : 2 * e + 2]
+            )
+        w1_codes = keep.tile([P, H], U32, name="w1_codes", align_bytes=64)
+        w1_sc = keep.tile([P, H], U8, name="w1_sc", align_bytes=64)
+        for t in range(2):
+            nc.vector.quantize_mx(
+                out=w1_codes[:, P * t : P * (t + 1)].bitcast(FP8X4), scales=w1_sc[:, P * t : P * (t + 1)],
+                in_=w1_bf[0][:, t, :],
+            )
+        nc.vector.quantize_mx(
+            out=w1_codes[:, 2 * P :].bitcast(FP8X4), scales=w1_sc[:, 2 * P :],
+            in_=w1_bf[1][:].rearrange("p t c -> p (t c)"),
+        )
 
         warm_bank = psum.tile([P, HALF], F32, name="warm_bank", tag="bank7")
-        for i in range(3):
+        for i in range(2):
             nc.tensor.matmul_mx(
                 out=warm_bank[:],
-                lhsT=w1_codes[:, 0:P].bitcast(FP8X4),
-                lhsT_scale=w1_sc[:, 0:P],
-                rhs=w1_codes[:].bitcast(FP8X4),
-                rhs_scale=w1_sc[:],
+                lhsT=x_codes[0][:, 0:P].bitcast(FP8X4),
+                lhsT_scale=x_sc[:, 0:P],
+                rhs=x_codes[1][:].bitcast(FP8X4),
+                rhs_scale=x_sc[:, HALF:],
                 start=True,
                 stop=True,
             )
 
         h = {}
-        for t, u in [(0, 0), (1, 0), (0, 1), (2, 0), (1, 1), (2, 1), (3, 0), (3, 1)]:
+        for t, u in [(0, 0), (0, 1), (1, 0), (1, 1), (2, 0), (2, 1), (3, 0), (3, 1)]:
             bank = psum.tile([P, HALF], F32, name=f"h{t}{u}", tag=f"bank{2 * t + u}")
             nc.tensor.matmul_mx(
                 out=bank[:],
@@ -111,14 +116,22 @@ def tile_picked_inorm_relu_p_kernel(tc, x_words, x_scales, w1, w2, gamma, offs, 
             h[t, u] = bank
 
         neg_gamma = keep.tile([P, PACK], F32, name="neg_gamma")
-        nc.scalar.activation(out=neg_gamma[:], in_=gamma_sb[:], func=ACT.Copy, scale=-1.0)
+        nc.gpsimd.tensor_scalar(out=neg_gamma[:], in0=gamma_sb[:], scalar1=-1.0, scalar2=0.0, op0=ALU.mult, op1=ALU.add)
+        w2_bf = keep.tile([P, N, PACK], BF16, name="w2_bf", align_bytes=64)
+        w2_cols = w2_raw[:].rearrange("p j n -> p n j")
+        for n0 in range(0, N, 64):
+            nc.gpsimd.tensor_scalar(
+                out=w2_bf[:, n0 : n0 + 64, :], in0=w2_cols[:, n0 : n0 + 64, :],
+                scalar1=1.0, scalar2=0.0, op0=ALU.mult, op1=ALU.add,
+            )
 
-        z_rows = [keep.tile([P, PACK, QUARTER], BF16, name=f"z_rows{c}", align_bytes=64) for c in range(4)]
+        z_rows = [keep.tile([P, 2, PACK, QUARTER], BF16, name=f"z_rows{u}", align_bytes=64) for u in range(2)]
         affine = [keep.tile([P, 3], F32, name=f"affine{t}") for t in range(PACK)]
+        rstd = [keep.tile([P, 1], F32, name=f"rstd{t}") for t in range(PACK)]
         shrunk = {}
 
         def stats_vector(t, u):
-            lo = 3 + 6 * u if t in (1, 3) else 3
+            lo = 3 if t in SCALAR_STATS else 3 + 6 * u
             nc.vector.bn_stats(out=stats[t][:, lo : lo + 6], in_=h[t, u][:])
 
         def stats_scalar(t):
@@ -126,7 +139,7 @@ def tile_picked_inorm_relu_p_kernel(tc, x_words, x_scales, w1, w2, gamma, offs, 
             nc.scalar.activation(
                 out=part[:], in_=h[t, 0][:], func=ACT.Copy, scale=1.0 / HALF, accum_out=stats[t][:, 1:2]
             )
-            squares = keep.tile([P, HALF], BF16, name=f"squares{t}", tag=f"scratch{t}", align_bytes=64)
+            squares = keep.tile([P, HALF], BF16, name=f"squares{t}", tag="squares", align_bytes=64)
             nc.scalar.activation(
                 out=squares[:], in_=h[t, 0][:], func=ACT.Square, scale=-1.0, bias=stats[t][:, 1:2],
                 accum_out=stats[t][:, 2:3],
@@ -134,124 +147,125 @@ def tile_picked_inorm_relu_p_kernel(tc, x_words, x_scales, w1, w2, gamma, offs, 
             shrunk[t] = part
 
         def aggregate(t):
-            tuples = stats[t][:, 3:15] if t in (1, 3) else stats[t][:, 0:9]
+            tuples = stats[t][:, 0:9] if t in SCALAR_STATS else stats[t][:, 3:15]
             nc.vector.bn_aggr(out=moments[t][:, 2:4], in_=tuples)
-            rstd = keep.tile([P, 1], F32, name=f"rstd{t}")
-            nc.scalar.activation(out=rstd[:], in_=moments[t][:, 3:4], func=ACT.Abs_reciprocal_sqrt, bias=EPS)
-            engine = nc.gpsimd if t == 0 else nc.vector
-            engine.tensor_scalar(
-                out=affine[t][:], in0=moments[t][:, 0:3], scalar1=neg_gamma[:, t : t + 1], scalar2=rstd[:],
+            nc.scalar.activation(out=rstd[t][:], in_=moments[t][:, 3:4], func=ACT.Abs_reciprocal_sqrt, bias=EPS)
+
+        def make_affine(t):
+            lo = 0 if t in SCALAR_STATS else 1
+            nc.vector.tensor_scalar(
+                out=affine[t][:, lo:3], in0=moments[t][:, lo:3], scalar1=neg_gamma[:, t : t + 1], scalar2=rstd[t][:],
                 op0=ALU.mult, op1=ALU.mult,
             )
 
-        def quarter_of(half_tile, c):
-            return half_tile[:, QUARTER * (c % 2) : QUARTER * (c % 2 + 1)]
-
-        def normalise_scalar(t, c):
+        def normalise_scalar(t, u, quarters=slice(0, 2)):
             nc.scalar.activation(
-                out=z_rows[c][:, t, :], in_=quarter_of(h[t, c // 2], c), func=ACT.Relu,
-                scale=affine[t][:, 1:2], bias=affine[t][:, 2:3],
+                out=z_rows[u][:, quarters, t, :], in_=h[t, u][:].rearrange("p (c n) -> p c n", c=2)[:, quarters],
+                func=ACT.Relu, scale=affine[t][:, 1:2], bias=affine[t][:, 2:3],
             )
 
         def normalise_vector(t, c):
-            source, col = (shrunk[t], 0) if t in shrunk else (h[t, 0], 1)
             nc.vector.tensor_scalar(
-                out=z_rows[c][:, t, :], in0=quarter_of(source, c), scalar1=affine[t][:, col : col + 1],
-                scalar2=affine[t][:, 2:3], op0=ALU.mult, op1=ALU.add,
+                out=z_rows[0][:, c, t, :], in0=shrunk[t][:, QUARTER * c : QUARTER * (c + 1)],
+                scalar1=affine[t][:, 0:1], scalar2=affine[t][:, 2:3], op0=ALU.mult, op1=ALU.add,
             )
-
-        stats_scalar(0)
-        stats_vector(1, 0)
-        stats_vector(0, 1)
-        aggregate(0)
-        stats_vector(1, 1)
-        aggregate(1)
-        stats_scalar(2)
-        stats_vector(2, 1)
-        aggregate(2)
-        stats_vector(3, 0)
-        stats_vector(3, 1)
-        aggregate(3)
-        w2_bf = keep.tile([P, N, PACK], BF16, name="w2_bf", tag="scratch0", align_bytes=64)
-        w2_cols = w2_raw[:].rearrange("p j n -> p n j")
-        for n0 in range(0, N, 64):
-            nc.gpsimd.tensor_scalar(
-                out=w2_bf[:, n0 : n0 + 64, :], in0=w2_cols[:, n0 : n0 + 64, :],
-                scalar1=1.0, scalar2=0.0, op0=ALU.mult, op1=ALU.add,
-            )
-        normalise_scalar(1, 0)
-        normalise_vector(0, 0)
-        normalise_vector(2, 0)
-        normalise_vector(3, 0)
-        for t in (1, 2, 3):
-            normalise_scalar(t, 1)
-        normalise_vector(0, 1)
-        for c in (3, 2):
-            for t in range(PACK):
-                normalise_scalar(t, c)
 
         w2_codes = keep.tile([P, N], U32, name="w2_codes", align_bytes=64)
         w2_sc = keep.tile([P, N], U8, name="w2_sc", align_bytes=64)
+
+        first, second = slice(0, 1), slice(1, 2)
+        stats_scalar(0)
+        stats_vector(0, 1)
+        stats_vector(1, 1)
+        aggregate(0)
+        stats_scalar(1)
+        stats_vector(2, 0)
+        make_affine(0)
+        stats_vector(2, 1)
+        aggregate(1)
+        normalise_scalar(0, 1)
+        stats_vector(3, 0)
+        aggregate(2)
+        make_affine(1)
+        normalise_scalar(1, 1)
+        stats_vector(3, 1)
+        make_affine(2)
+        normalise_scalar(2, 0)
+        aggregate(3)
+        normalise_vector(0, 0)
+        normalise_vector(1, 0)
+        make_affine(3)
+        normalise_scalar(2, 1, first)
+        normalise_scalar(3, 0, first)
+        normalise_scalar(3, 0, second)
+        normalise_scalar(2, 1, second)
+        normalise_scalar(3, 1)
         nc.vector.quantize_mx(out=w2_codes[:].bitcast(FP8X4), scales=w2_sc[:], in_=w2_bf[:].rearrange("p n j -> p (n j)"))
 
-        z_bf = [keep.tile([P, QUARTER * PACK], BF16, name=f"z_bf{c}", align_bytes=64) for c in range(4)]
-        z_codes = [keep.tile([P, QUARTER], U32, name=f"z_codes{c}", align_bytes=64) for c in range(4)]
-        z_sc = [keep.tile([P, QUARTER], U8, name=f"z_sc{c}", align_bytes=64) for c in range(4)]
+        pieces = [(0, 0, 256), (1, 0, 256), (2, 0, 128), (2, 128, 128), (3, 0, 128), (3, 128, 128)]
+        z_bf = [keep.tile([P, w * PACK], BF16, name=f"z_bf{i}", align_bytes=64) for i, (c, lo, w) in enumerate(pieces)]
+        z_codes = [keep.tile([P, w], U32, name=f"z_codes{i}", align_bytes=64) for i, (c, lo, w) in enumerate(pieces)]
+        z_sc = [keep.tile([P, w], U8, name=f"z_sc{i}", align_bytes=64) for i, (c, lo, w) in enumerate(pieces)]
 
-        def rows_of(c):
-            return z_rows[c][:].rearrange("p t (g i) -> p g t i", i=4)
+        def interleave(i):
+            c, lo, w = pieces[i]
+            nc.vector.tensor_scalar_max(
+                out=z_bf[i][:].rearrange("p (g i t) -> p g t i", i=4, t=PACK),
+                in0=z_rows[c // 2][:, c % 2, :, lo : lo + w].rearrange("p t (g i) -> p g t i", i=4),
+                scalar1=0.0,
+            )
 
-        def words_of(c):
-            return z_bf[c][:].rearrange("p (g i t) -> p g t i", i=4, t=PACK)
+        def quantise(i):
+            nc.vector.quantize_mx(out=z_codes[i][:].bitcast(FP8X4), scales=z_sc[i][:], in_=z_bf[i][:])
 
-        def interleave_vector(c, groups=slice(0, QUARTER // 4)):
-            nc.vector.tensor_scalar_max(out=words_of(c)[:, groups], in0=rows_of(c)[:, groups], scalar1=0.0)
-
-        def interleave_scalar(c, groups):
-            nc.scalar.copy(out=words_of(c)[:, groups], in_=rows_of(c)[:, groups])
-
-        def quantise(c):
-            nc.vector.quantize_mx(out=z_codes[c][:].bitcast(FP8X4), scales=z_sc[c][:], in_=z_bf[c][:])
-
-        def product(c, m, acc):
+        def product(i, m, acc):
             nc.tensor.matmul_mx(
                 out=acc,
                 lhsT=w2_codes[:, P * m : P * (m + 1)].bitcast(FP8X4),
                 lhsT_scale=w2_sc[:, P * m : P * (m + 1)],
-                rhs=z_codes[c][:].bitcast(FP8X4),
-                rhs_scale=z_sc[c][:],
+                rhs=z_codes[i][:].bitcast(FP8X4),
+                rhs_scale=z_sc[i][:],
                 start=True,
                 stop=True,
             )
 
-        def second_layer(c):
-            acc = psum.tile([P, 2, QUARTER], F32, name=f"acc{c}", tag=f"bank{(0, 4, 2, 2)[c]}")
+        def second_layer(i, bank):
+            c, lo, w = pieces[i]
+            acc = psum.tile([P, 2, w], F32, name=f"acc{i}", tag=f"bank{bank}")
             for m in range(2):
-                product(c, m, acc[:, m, :])
-            res = keep.tile([P, 2, QUARTER], F32, name=f"res{c}")
+                product(i, m, acc[:, m, :])
+            res = keep.tile([P, 2, w], F32, name=f"res{i}")
             nc.scalar.copy(out=res[:], in_=acc[:])
-            nc.sync.dma_start(
-                out=out[:, QUARTER * c : QUARTER * (c + 1)].rearrange("(m p) n -> p m n", p=P), in_=res[:]
-            )
+            col = QUARTER * c + lo
+            nc.sync.dma_start(out=out[:, col : col + w].rearrange("(m p) n -> p m n", p=P), in_=res[:])
 
-        def last_second_layer(c):
+        def last_second_layer(i, banks):
+            c, lo, w = pieces[i]
+            col = QUARTER * c + lo
             for m, engine_copy in enumerate((nc.scalar.copy, nc.vector.tensor_copy)):
-                acc = psum.tile([P, QUARTER], F32, name=f"acc{c}{m}", tag=f"bank{2 * m + 1}")
-                product(c, m, acc[:])
-                res = keep.tile([P, QUARTER], F32, name=f"res{c}{m}")
+                acc = psum.tile([P, w], F32, name=f"acc{i}{m}", tag=f"bank{banks[m]}")
+                product(i, m, acc[:])
+                res = keep.tile([P, w], F32, name=f"res{i}{m}")
                 engine_copy(out=res[:], in_=acc[:])
-                nc.sync.dma_start(out=out[P * m : P * (m + 1), QUARTER * c : QUARTER * (c + 1)], in_=res[:])
+                nc.sync.dma_start(out=out[P * m : P * (m + 1), col : col + w], in_=res[:])
 
-        interleave_vector(0)
-        interleave_vector(1)
+        interleave(0)
+        normalise_vector(0, 1)
+        normalise_vector(1, 1)
         quantise(0)
+        second_layer(0, 0)
+        interleave(1)
+        interleave(2)
         quantise(1)
-        interleave_scalar(3, slice(0, QUARTER // 8))
-        second_layer(0)
-        second_layer(1)
-        interleave_vector(3, slice(QUARTER // 8, QUARTER // 4))
-        interleave_vector(2)
-        quantise(3)
+        second_layer(1, 2)
+        interleave(3)
         quantise(2)
-        second_layer(3)
-        last_second_layer(2)
+        second_layer(2, 4)
+        interleave(4)
+        quantise(3)
+        second_layer(3, 6)
+        interleave(5)
+        quantise(4)
+        second_layer(4, 5)
+        quantise(5)
+        last_second_layer(5, (1, 3))

@@ -21,7 +21,7 @@ PACK = 4
 HALF = 512
 QUARTER = 256
 FIRST_COLS = 1024
-SCALAR_STATS = (0, 1)
+SCALAR_STATS = (0, 2)
 
 
 def tile_picked_inorm_relu_p_kernel(tc, x_words, x_scales, w1, w2, gamma, offs, out):
@@ -32,9 +32,8 @@ def tile_picked_inorm_relu_p_kernel(tc, x_words, x_scales, w1, w2, gamma, offs, 
 
         offsets = keep.tile([P, S // 16], U16, name="offsets")
         table_words = keep.tile([P, T], U32, name="table_words", align_bytes=64)
-        table_scales = keep.tile([P, T], U8, name="table_scales", align_bytes=64)
-        w1_raw = keep.tile([P, PACK, H], F32, name="w1_raw")
-        w2_raw = keep.tile([P, PACK, N], F32, name="w2_raw")
+        table_scales = keep.tile([P, T], U8, name="table_scales", tag="scales_then_w2", align_bytes=64)
+        w1_raw = [keep.tile([P, 2, H], F32, name=f"w1_raw{a}") for a in range(2)]
         gamma_sb = keep.tile([P, PACK], F32, name="gamma_sb")
 
         nc.vector.memset(table_scales[:].bitcast(I32), 0)
@@ -43,8 +42,9 @@ def tile_picked_inorm_relu_p_kernel(tc, x_words, x_scales, w1, w2, gamma, offs, 
         nc.sync.dma_start(offsets[:], offs)
         nc.sync.dma_start(out=table_scales[0:P:8, :].bitcast(I32), in_=x_scales[0].bitcast(I32))
         nc.sync.dma_start(out=table_words[:, FIRST_COLS:].bitcast(I32), in_=words[:, FIRST_COLS:])
-        nc.sync.dma_start(out=w1_raw[:], in_=w1.rearrange("(p j) c -> p j c", j=PACK))
-        nc.sync.dma_start(out=w2_raw[:], in_=w2.rearrange("(p j) c -> p j c", j=PACK))
+        w1_rows = w1.rearrange("(p j) c -> p j c", j=PACK)
+        for a in range(2):
+            nc.sync.dma_start(out=w1_raw[a][:], in_=w1_rows[:, 2 * a : 2 * a + 2, :])
         nc.sync.dma_start(out=gamma_sb[:], in_=gamma.rearrange("(p t) o -> p (t o)", t=PACK))
 
         warm_in = keep.tile([P, 1], F32, name="warm_in")
@@ -55,28 +55,32 @@ def tile_picked_inorm_relu_p_kernel(tc, x_words, x_scales, w1, w2, gamma, offs, 
         stats = [keep.tile([P, 15], F32, name=f"stats{t}") for t in range(PACK)]
         moments = [keep.tile([P, 4], F32, name=f"moments{t}") for t in range(PACK)]
         for t in range(PACK):
-            if t in SCALAR_STATS:
-                nc.vector.memset(moments[t][:, 0:1], -float(HALF))
-                nc.vector.memset(stats[t][:, 0:1], float(HALF))
+            nc.vector.memset(moments[t][:, 0:1], -float(HALF))
             nc.vector.memset(moments[t][:, 1:2], -1.0)
+        for t in SCALAR_STATS:
+            nc.vector.memset(stats[t][:, 0:1], float(HALF))
 
         picked_sc = keep.tile([P, S], U8, name="picked_sc", align_bytes=64)
-        nc.vector.tensor_copy(picked_sc[:], table_scales[:].indirect(offsets[:]))
         x_sc = keep.tile([P, S], U8, name="x_sc", align_bytes=64)
+        nc.vector.tensor_copy(picked_sc[:], table_scales[:].indirect(offsets[:]))
         nc.vector.tensor_copy(x_sc[:].bitcast(I32), picked_sc[:].bitcast(I32))
         for r in range(1, 4):
             nc.scalar.dma_start(out=x_sc[r:P:32, :].bitcast(I32), in_=picked_sc[8 * r : P : 32, :].bitcast(I32))
+        w2_raw = keep.tile([P, PACK, N], F32, name="w2_raw", tag="scales_then_w2", align_bytes=64)
+        nc.sync.dma_start(out=w2_raw[:], in_=w2.rearrange("(p j) c -> p j c", j=PACK))
 
         x_codes = [keep.tile([P, HALF], U32, name=f"x_codes{u}", align_bytes=64) for u in range(2)]
         for u in range(2):
             nc.vector.tensor_copy(x_codes[u][:], table_words[:].indirect(offsets[:, 32 * u : 32 * (u + 1)]))
 
         w1_bf = [keep.tile([P, 2, P * PACK], BF16, name=f"w1_bf{e}", align_bytes=64) for e in range(2)]
-        w1_cols = w1_raw[:].rearrange("p j (m t) -> p m j t", t=PACK)
-        for e, engine_copy in enumerate((nc.vector.tensor_copy, nc.scalar.copy)):
-            engine_copy(
-                out=w1_bf[e][:].rearrange("p t (m j) -> p m j t", j=PACK), in_=w1_cols[:, :, :, 2 * e : 2 * e + 2]
-            )
+        for a, engine_copy in enumerate((nc.scalar.copy, nc.vector.tensor_copy)):
+            w1_cols = w1_raw[a][:].rearrange("p j (m t) -> p m j t", t=PACK)
+            for e in range(2):
+                engine_copy(
+                    out=w1_bf[e][:].rearrange("p t (m j) -> p m j t", j=PACK)[:, :, 2 * a : 2 * a + 2, :],
+                    in_=w1_cols[:, :, :, 2 * e : 2 * e + 2],
+                )
         w1_codes = keep.tile([P, H], U32, name="w1_codes", align_bytes=64)
         w1_sc = keep.tile([P, H], U8, name="w1_sc", align_bytes=64)
         for t in range(2):
@@ -94,15 +98,15 @@ def tile_picked_inorm_relu_p_kernel(tc, x_words, x_scales, w1, w2, gamma, offs, 
             nc.tensor.matmul_mx(
                 out=warm_bank[:],
                 lhsT=x_codes[0][:, 0:P].bitcast(FP8X4),
-                lhsT_scale=x_sc[:, 0:P],
-                rhs=x_codes[1][:].bitcast(FP8X4),
-                rhs_scale=x_sc[:, HALF:],
+                lhsT_scale=picked_sc[:, 0:P],
+                rhs=x_codes[0][:].bitcast(FP8X4),
+                rhs_scale=picked_sc[:, :HALF],
                 start=True,
                 stop=True,
             )
 
         h = {}
-        for t, u in [(0, 0), (0, 1), (1, 0), (1, 1), (2, 0), (2, 1), (3, 0), (3, 1)]:
+        for t, u in [(0, 0), (1, 0), (0, 1), (2, 0), (1, 1), (2, 1), (3, 0), (3, 1)]:
             bank = psum.tile([P, HALF], F32, name=f"h{t}{u}", tag=f"bank{2 * t + u}")
             nc.tensor.matmul_mx(
                 out=bank[:],
@@ -116,22 +120,14 @@ def tile_picked_inorm_relu_p_kernel(tc, x_words, x_scales, w1, w2, gamma, offs, 
             h[t, u] = bank
 
         neg_gamma = keep.tile([P, PACK], F32, name="neg_gamma")
-        nc.gpsimd.tensor_scalar(out=neg_gamma[:], in0=gamma_sb[:], scalar1=-1.0, scalar2=0.0, op0=ALU.mult, op1=ALU.add)
-        w2_bf = keep.tile([P, N, PACK], BF16, name="w2_bf", align_bytes=64)
-        w2_cols = w2_raw[:].rearrange("p j n -> p n j")
-        for n0 in range(0, N, 64):
-            nc.gpsimd.tensor_scalar(
-                out=w2_bf[:, n0 : n0 + 64, :], in0=w2_cols[:, n0 : n0 + 64, :],
-                scalar1=1.0, scalar2=0.0, op0=ALU.mult, op1=ALU.add,
-            )
+        nc.scalar.activation(out=neg_gamma[:], in_=gamma_sb[:], func=ACT.Copy, scale=-1.0)
 
-        z_rows = [keep.tile([P, 2, PACK, QUARTER], BF16, name=f"z_rows{u}", align_bytes=64) for u in range(2)]
+        z_rows = [keep.tile([P, PACK, QUARTER], BF16, name=f"z_rows{c}", align_bytes=64) for c in range(4)]
         affine = [keep.tile([P, 3], F32, name=f"affine{t}") for t in range(PACK)]
-        rstd = [keep.tile([P, 1], F32, name=f"rstd{t}") for t in range(PACK)]
         shrunk = {}
 
         def stats_vector(t, u):
-            lo = 3 if t in SCALAR_STATS else 3 + 6 * u
+            lo = 3 + 6 * u if t in (1, 3) else 3
             nc.vector.bn_stats(out=stats[t][:, lo : lo + 6], in_=h[t, u][:])
 
         def stats_scalar(t):
@@ -139,7 +135,7 @@ def tile_picked_inorm_relu_p_kernel(tc, x_words, x_scales, w1, w2, gamma, offs, 
             nc.scalar.activation(
                 out=part[:], in_=h[t, 0][:], func=ACT.Copy, scale=1.0 / HALF, accum_out=stats[t][:, 1:2]
             )
-            squares = keep.tile([P, HALF], BF16, name=f"squares{t}", tag="squares", align_bytes=64)
+            squares = keep.tile([P, HALF], BF16, name=f"squares{t}", tag=f"scratch{t}", align_bytes=64)
             nc.scalar.activation(
                 out=squares[:], in_=h[t, 0][:], func=ACT.Square, scale=-1.0, bias=stats[t][:, 1:2],
                 accum_out=stats[t][:, 2:3],
@@ -147,125 +143,124 @@ def tile_picked_inorm_relu_p_kernel(tc, x_words, x_scales, w1, w2, gamma, offs, 
             shrunk[t] = part
 
         def aggregate(t):
-            tuples = stats[t][:, 0:9] if t in SCALAR_STATS else stats[t][:, 3:15]
+            tuples = stats[t][:, 3:15] if t in (1, 3) else stats[t][:, 0:9]
             nc.vector.bn_aggr(out=moments[t][:, 2:4], in_=tuples)
-            nc.scalar.activation(out=rstd[t][:], in_=moments[t][:, 3:4], func=ACT.Abs_reciprocal_sqrt, bias=EPS)
-
-        def make_affine(t):
-            lo = 0 if t in SCALAR_STATS else 1
-            nc.vector.tensor_scalar(
-                out=affine[t][:, lo:3], in0=moments[t][:, lo:3], scalar1=neg_gamma[:, t : t + 1], scalar2=rstd[t][:],
+            rstd = keep.tile([P, 1], F32, name=f"rstd{t}")
+            nc.scalar.activation(out=rstd[:], in_=moments[t][:, 3:4], func=ACT.Abs_reciprocal_sqrt, bias=EPS)
+            engine = nc.gpsimd if t == 0 else nc.vector
+            engine.tensor_scalar(
+                out=affine[t][:], in0=moments[t][:, 0:3], scalar1=neg_gamma[:, t : t + 1], scalar2=rstd[:],
                 op0=ALU.mult, op1=ALU.mult,
             )
 
-        def normalise_scalar(t, u, quarters=slice(0, 2)):
+        def quarter_of(half_tile, c):
+            return half_tile[:, QUARTER * (c % 2) : QUARTER * (c % 2 + 1)]
+
+        def normalise_scalar(t, c):
             nc.scalar.activation(
-                out=z_rows[u][:, quarters, t, :], in_=h[t, u][:].rearrange("p (c n) -> p c n", c=2)[:, quarters],
-                func=ACT.Relu, scale=affine[t][:, 1:2], bias=affine[t][:, 2:3],
+                out=z_rows[c][:, t, :], in_=quarter_of(h[t, c // 2], c), func=ACT.Relu,
+                scale=affine[t][:, 1:2], bias=affine[t][:, 2:3],
             )
 
         def normalise_vector(t, c):
+            source, col = (shrunk[t], 0) if t in shrunk else (h[t, 0], 1)
             nc.vector.tensor_scalar(
-                out=z_rows[0][:, c, t, :], in0=shrunk[t][:, QUARTER * c : QUARTER * (c + 1)],
-                scalar1=affine[t][:, 0:1], scalar2=affine[t][:, 2:3], op0=ALU.mult, op1=ALU.add,
+                out=z_rows[c][:, t, :], in0=quarter_of(source, c), scalar1=affine[t][:, col : col + 1],
+                scalar2=affine[t][:, 2:3], op0=ALU.mult, op1=ALU.add,
             )
+
+        stats_scalar(0)
+        stats_vector(1, 0)
+        stats_vector(0, 1)
+        aggregate(0)
+        stats_vector(1, 1)
+        aggregate(1)
+        stats_scalar(2)
+        stats_vector(2, 1)
+        aggregate(2)
+        stats_vector(3, 0)
+        stats_vector(3, 1)
+        aggregate(3)
+        w2_bf = keep.tile([P, N, PACK], BF16, name="w2_bf", tag="scratch0", align_bytes=64)
+        w2_cols = w2_raw[:].rearrange("p j n -> p n j")
+        for n0 in range(0, N, 64):
+            nc.gpsimd.tensor_scalar(
+                out=w2_bf[:, n0 : n0 + 64, :], in0=w2_cols[:, n0 : n0 + 64, :],
+                scalar1=1.0, scalar2=0.0, op0=ALU.mult, op1=ALU.add,
+            )
+        normalise_scalar(1, 0)
+        normalise_vector(0, 0)
+        normalise_vector(2, 0)
+        normalise_vector(3, 0)
+        for t in (1, 2, 3):
+            normalise_scalar(t, 1)
+        normalise_vector(0, 1)
+        for c in (3, 2):
+            for t in range(PACK):
+                normalise_scalar(t, c)
 
         w2_codes = keep.tile([P, N], U32, name="w2_codes", align_bytes=64)
         w2_sc = keep.tile([P, N], U8, name="w2_sc", align_bytes=64)
-
-        first, second = slice(0, 1), slice(1, 2)
-        stats_scalar(0)
-        stats_vector(0, 1)
-        stats_vector(1, 1)
-        aggregate(0)
-        stats_scalar(1)
-        stats_vector(2, 0)
-        make_affine(0)
-        stats_vector(2, 1)
-        aggregate(1)
-        normalise_scalar(0, 1)
-        stats_vector(3, 0)
-        aggregate(2)
-        make_affine(1)
-        normalise_scalar(1, 1)
-        stats_vector(3, 1)
-        make_affine(2)
-        normalise_scalar(2, 0)
-        aggregate(3)
-        normalise_vector(0, 0)
-        normalise_vector(1, 0)
-        make_affine(3)
-        normalise_scalar(2, 1, first)
-        normalise_scalar(3, 0, first)
-        normalise_scalar(3, 0, second)
-        normalise_scalar(2, 1, second)
-        normalise_scalar(3, 1)
         nc.vector.quantize_mx(out=w2_codes[:].bitcast(FP8X4), scales=w2_sc[:], in_=w2_bf[:].rearrange("p n j -> p (n j)"))
 
-        pieces = [(0, 0, 256), (1, 0, 256), (2, 0, 128), (2, 128, 128), (3, 0, 128), (3, 128, 128)]
-        z_bf = [keep.tile([P, w * PACK], BF16, name=f"z_bf{i}", align_bytes=64) for i, (c, lo, w) in enumerate(pieces)]
-        z_codes = [keep.tile([P, w], U32, name=f"z_codes{i}", align_bytes=64) for i, (c, lo, w) in enumerate(pieces)]
-        z_sc = [keep.tile([P, w], U8, name=f"z_sc{i}", align_bytes=64) for i, (c, lo, w) in enumerate(pieces)]
+        z_bf = [keep.tile([P, QUARTER * PACK], BF16, name=f"z_bf{c}", align_bytes=64) for c in range(4)]
+        z_codes = [keep.tile([P, QUARTER], U32, name=f"z_codes{c}", align_bytes=64) for c in range(4)]
+        z_sc = [keep.tile([P, QUARTER], U8, name=f"z_sc{c}", align_bytes=64) for c in range(4)]
 
-        def interleave(i):
-            c, lo, w = pieces[i]
-            nc.vector.tensor_scalar_max(
-                out=z_bf[i][:].rearrange("p (g i t) -> p g t i", i=4, t=PACK),
-                in0=z_rows[c // 2][:, c % 2, :, lo : lo + w].rearrange("p t (g i) -> p g t i", i=4),
-                scalar1=0.0,
-            )
+        def rows_of(c):
+            return z_rows[c][:].rearrange("p t (g i) -> p g t i", i=4)
 
-        def quantise(i):
-            nc.vector.quantize_mx(out=z_codes[i][:].bitcast(FP8X4), scales=z_sc[i][:], in_=z_bf[i][:])
+        def words_of(c):
+            return z_bf[c][:].rearrange("p (g i t) -> p g t i", i=4, t=PACK)
 
-        def product(i, m, acc):
+        def interleave_vector(c, groups=slice(0, QUARTER // 4)):
+            nc.vector.tensor_scalar_max(out=words_of(c)[:, groups], in0=rows_of(c)[:, groups], scalar1=0.0)
+
+        def interleave_scalar(c, groups):
+            nc.scalar.copy(out=words_of(c)[:, groups], in_=rows_of(c)[:, groups])
+
+        def quantise(c):
+            nc.vector.quantize_mx(out=z_codes[c][:].bitcast(FP8X4), scales=z_sc[c][:], in_=z_bf[c][:])
+
+        def product(c, m, acc):
             nc.tensor.matmul_mx(
                 out=acc,
                 lhsT=w2_codes[:, P * m : P * (m + 1)].bitcast(FP8X4),
                 lhsT_scale=w2_sc[:, P * m : P * (m + 1)],
-                rhs=z_codes[i][:].bitcast(FP8X4),
-                rhs_scale=z_sc[i][:],
+                rhs=z_codes[c][:].bitcast(FP8X4),
+                rhs_scale=z_sc[c][:],
                 start=True,
                 stop=True,
             )
 
-        def second_layer(i, bank):
-            c, lo, w = pieces[i]
-            acc = psum.tile([P, 2, w], F32, name=f"acc{i}", tag=f"bank{bank}")
+        def second_layer(c):
+            acc = psum.tile([P, 2, QUARTER], F32, name=f"acc{c}", tag=f"bank{(0, 4, 2, 2)[c]}")
             for m in range(2):
-                product(i, m, acc[:, m, :])
-            res = keep.tile([P, 2, w], F32, name=f"res{i}")
+                product(c, m, acc[:, m, :])
+            res = keep.tile([P, 2, QUARTER], F32, name=f"res{c}")
             nc.scalar.copy(out=res[:], in_=acc[:])
-            col = QUARTER * c + lo
-            nc.sync.dma_start(out=out[:, col : col + w].rearrange("(m p) n -> p m n", p=P), in_=res[:])
+            nc.sync.dma_start(
+                out=out[:, QUARTER * c : QUARTER * (c + 1)].rearrange("(m p) n -> p m n", p=P), in_=res[:]
+            )
 
-        def last_second_layer(i, banks):
-            c, lo, w = pieces[i]
-            col = QUARTER * c + lo
+        def last_second_layer(c):
             for m, engine_copy in enumerate((nc.scalar.copy, nc.vector.tensor_copy)):
-                acc = psum.tile([P, w], F32, name=f"acc{i}{m}", tag=f"bank{banks[m]}")
-                product(i, m, acc[:])
-                res = keep.tile([P, w], F32, name=f"res{i}{m}")
+                acc = psum.tile([P, QUARTER], F32, name=f"acc{c}{m}", tag=f"bank{2 * m + 1}")
+                product(c, m, acc[:])
+                res = keep.tile([P, QUARTER], F32, name=f"res{c}{m}")
                 engine_copy(out=res[:], in_=acc[:])
-                nc.sync.dma_start(out=out[P * m : P * (m + 1), col : col + w], in_=res[:])
+                nc.sync.dma_start(out=out[P * m : P * (m + 1), QUARTER * c : QUARTER * (c + 1)], in_=res[:])
 
-        interleave(0)
-        normalise_vector(0, 1)
-        normalise_vector(1, 1)
+        interleave_vector(0)
+        interleave_vector(1)
         quantise(0)
-        second_layer(0, 0)
-        interleave(1)
-        interleave(2)
         quantise(1)
-        second_layer(1, 2)
-        interleave(3)
-        quantise(2)
-        second_layer(2, 4)
-        interleave(4)
+        interleave_scalar(3, slice(0, QUARTER // 8))
+        second_layer(0)
+        second_layer(1)
+        interleave_vector(3, slice(QUARTER // 8, QUARTER // 4))
+        interleave_vector(2)
         quantise(3)
-        second_layer(3, 6)
-        interleave(5)
-        quantise(4)
-        second_layer(4, 5)
-        quantise(5)
-        last_second_layer(5, (1, 3))
+        quantise(2)
+        second_layer(3)
+        last_second_layer(2)

@@ -195,72 +195,94 @@ def tile_picked_inorm_relu_p_kernel(tc, x_words, x_scales, w1, w2, gamma, offs, 
         for t in (1, 2, 3):
             normalise_scalar(t, 1)
         normalise_vector(0, 1)
-        for c in (3, 2):
-            for t in range(PACK):
-                normalise_scalar(t, c)
+        for t in range(PACK):
+            normalise_scalar(t, 3)
 
         w2_codes = keep.tile([P, N], U32, name="w2_codes", align_bytes=64)
         w2_sc = keep.tile([P, N], U8, name="w2_sc", align_bytes=64)
-        nc.vector.quantize_mx(out=w2_codes[:].bitcast(FP8X4), scales=w2_sc[:], in_=w2_bf[:].rearrange("p n j -> p (n j)"))
 
-        z_bf = [keep.tile([P, QUARTER * PACK], BF16, name=f"z_bf{c}", align_bytes=64) for c in range(4)]
-        z_codes = [keep.tile([P, QUARTER], U32, name=f"z_codes{c}", align_bytes=64) for c in range(4)]
-        z_sc = [keep.tile([P, QUARTER], U8, name=f"z_sc{c}", align_bytes=64) for c in range(4)]
+        pieces = [(c, lo, 128) for c in (0, 1, 3, 2) for lo in (0, 128)]
+        z_codes = [
+            keep.tile([P, w], U32, name=f"z_codes{i}", tag=f"z_codes{i}", align_bytes=64)
+            for i, (c, lo, w) in enumerate(pieces)
+        ]
+        z_bf = [
+            keep.tile([P, w * PACK], BF16, name=f"z_bf{i}", tag="z_codes0" if i == 4 else f"z_bf{i}", align_bytes=64)
+            for i, (c, lo, w) in enumerate(pieces)
+        ]
+        z_sc = [keep.tile([P, w], U8, name=f"z_sc{i}", align_bytes=64) for i, (c, lo, w) in enumerate(pieces)]
 
-        def rows_of(c):
-            return z_rows[c][:].rearrange("p t (g i) -> p g t i", i=4)
+        def rows_of(i):
+            c, lo, w = pieces[i]
+            return z_rows[c][:, :, lo : lo + w].rearrange("p t (g i) -> p g t i", i=4)
 
-        def words_of(c):
-            return z_bf[c][:].rearrange("p (g i t) -> p g t i", i=4, t=PACK)
+        def words_of(i):
+            return z_bf[i][:].rearrange("p (g i t) -> p g t i", i=4, t=PACK)
 
-        def interleave_vector(c, groups=slice(0, QUARTER // 4)):
-            nc.vector.tensor_scalar_max(out=words_of(c)[:, groups], in0=rows_of(c)[:, groups], scalar1=0.0)
+        def interleave_vector(i):
+            nc.vector.tensor_scalar_max(out=words_of(i), in0=rows_of(i), scalar1=0.0)
 
-        def interleave_scalar(c, groups):
-            nc.scalar.copy(out=words_of(c)[:, groups], in_=rows_of(c)[:, groups])
+        def interleave_scalar(i):
+            nc.scalar.copy(out=words_of(i), in_=rows_of(i))
 
-        def quantise(c):
-            nc.vector.quantize_mx(out=z_codes[c][:].bitcast(FP8X4), scales=z_sc[c][:], in_=z_bf[c][:])
+        def quantise(i):
+            nc.vector.quantize_mx(out=z_codes[i][:].bitcast(FP8X4), scales=z_sc[i][:], in_=z_bf[i][:])
 
-        def product(c, m, acc):
+        def product(i, m, acc):
             nc.tensor.matmul_mx(
                 out=acc,
                 lhsT=w2_codes[:, P * m : P * (m + 1)].bitcast(FP8X4),
                 lhsT_scale=w2_sc[:, P * m : P * (m + 1)],
-                rhs=z_codes[c][:].bitcast(FP8X4),
-                rhs_scale=z_sc[c][:],
+                rhs=z_codes[i][:].bitcast(FP8X4),
+                rhs_scale=z_sc[i][:],
                 start=True,
                 stop=True,
             )
 
-        def second_layer(c):
-            acc = psum.tile([P, 2, QUARTER], F32, name=f"acc{c}", tag=f"bank{(0, 4, 2, 2)[c]}")
+        def second_layer(i, bank, engine_copy):
+            c, lo, w = pieces[i]
+            col = QUARTER * c + lo
+            acc = psum.tile([P, 2, w], F32, name=f"acc{i}", tag=f"bank{bank}")
             for m in range(2):
-                product(c, m, acc[:, m, :])
-            res = keep.tile([P, 2, QUARTER], F32, name=f"res{c}")
-            nc.scalar.copy(out=res[:], in_=acc[:])
-            nc.sync.dma_start(
-                out=out[:, QUARTER * c : QUARTER * (c + 1)].rearrange("(m p) n -> p m n", p=P), in_=res[:]
-            )
+                product(i, m, acc[:, m, :])
+            res = keep.tile([P, 2, w], F32, name=f"res{i}")
+            engine_copy(out=res[:], in_=acc[:])
+            nc.sync.dma_start(out=out[:, col : col + w].rearrange("(m p) n -> p m n", p=P), in_=res[:])
 
-        def last_second_layer(c):
+        def shared_second_layer(i, banks):
+            c, lo, w = pieces[i]
+            col = QUARTER * c + lo
             for m, engine_copy in enumerate((nc.scalar.copy, nc.vector.tensor_copy)):
-                acc = psum.tile([P, QUARTER], F32, name=f"acc{c}{m}", tag=f"bank{2 * m + 1}")
-                product(c, m, acc[:])
-                res = keep.tile([P, QUARTER], F32, name=f"res{c}{m}")
+                acc = psum.tile([P, w], F32, name=f"acc{i}{m}", tag=f"bank{banks[m]}")
+                product(i, m, acc[:])
+                res = keep.tile([P, w], F32, name=f"res{i}{m}")
                 engine_copy(out=res[:], in_=acc[:])
-                nc.sync.dma_start(out=out[P * m : P * (m + 1), QUARTER * c : QUARTER * (c + 1)], in_=res[:])
+                nc.sync.dma_start(out=out[P * m : P * (m + 1), col : col + w], in_=res[:])
 
+        nc.vector.quantize_mx(out=w2_codes[:].bitcast(FP8X4), scales=w2_sc[:], in_=w2_bf[:].rearrange("p n j -> p (n j)"))
         interleave_vector(0)
         interleave_vector(1)
         quantise(0)
-        quantise(1)
-        interleave_scalar(3, slice(0, QUARTER // 8))
-        second_layer(0)
-        second_layer(1)
-        interleave_vector(3, slice(QUARTER // 8, QUARTER // 4))
+        second_layer(0, 0, nc.scalar.copy)
         interleave_vector(2)
-        quantise(3)
+        quantise(1)
+        second_layer(1, 4, nc.scalar.copy)
+        interleave_vector(3)
         quantise(2)
-        second_layer(3)
-        last_second_layer(2)
+        second_layer(2, 2, nc.scalar.copy)
+        for t in range(PACK):
+            normalise_scalar(t, 2)
+        interleave_scalar(4)
+        interleave_vector(5)
+        quantise(3)
+        second_layer(3, 6, nc.scalar.copy)
+        interleave_vector(6)
+        quantise(5)
+        second_layer(5, 0, nc.scalar.copy)
+        quantise(4)
+        second_layer(4, 4, nc.scalar.copy)
+        interleave_vector(7)
+        quantise(6)
+        second_layer(6, 1, nc.scalar.copy)
+        quantise(7)
+        shared_second_layer(7, (3, 5))

@@ -62,10 +62,10 @@ def tile_picked_inorm_relu_p_kernel(tc, x_words, x_scales, w1, w2, gamma, offs, 
 
         picked_sc = keep.tile([P, S], U8, name="picked_sc", align_bytes=64)
         x_sc = keep.tile([P, S], U8, name="x_sc", align_bytes=64)
+        nc.vector.memset(x_sc[:].bitcast(I32), 0)
         nc.vector.tensor_copy(picked_sc[:], table_scales[:].indirect(offsets[:]))
-        nc.vector.tensor_copy(x_sc[:].bitcast(I32), picked_sc[:].bitcast(I32))
-        for r in range(1, 4):
-            nc.scalar.dma_start(out=x_sc[r:P:32, :].bitcast(I32), in_=picked_sc[8 * r : P : 32, :].bitcast(I32))
+        for r in range(4):
+            nc.sync.dma_start(out=x_sc[r:P:32, :].bitcast(I32), in_=picked_sc[8 * r : P : 32, :].bitcast(I32))
         w2_raw = keep.tile([P, PACK, N], F32, name="w2_raw", tag="scales_then_w2", align_bytes=64)
         nc.sync.dma_start(out=w2_raw[:], in_=w2.rearrange("(p j) c -> p j c", j=PACK))
 
@@ -74,13 +74,16 @@ def tile_picked_inorm_relu_p_kernel(tc, x_words, x_scales, w1, w2, gamma, offs, 
             nc.vector.tensor_copy(x_codes[u][:], table_words[:].indirect(offsets[:, 32 * u : 32 * (u + 1)]))
 
         w1_bf = [keep.tile([P, 2, P * PACK], BF16, name=f"w1_bf{e}", align_bytes=64) for e in range(2)]
-        for a, engine_copy in enumerate((nc.scalar.copy, nc.vector.tensor_copy)):
-            w1_cols = w1_raw[a][:].rearrange("p j (m t) -> p m j t", t=PACK)
-            for e in range(2):
-                engine_copy(
-                    out=w1_bf[e][:].rearrange("p t (m j) -> p m j t", j=PACK)[:, :, 2 * a : 2 * a + 2, :],
-                    in_=w1_cols[:, :, :, 2 * e : 2 * e + 2],
-                )
+        def round_w1(engine_copy, a, e):
+            engine_copy(
+                out=w1_bf[e][:].rearrange("p t (m j) -> p m j t", j=PACK)[:, :, 2 * a : 2 * a + 2, :],
+                in_=w1_raw[a][:].rearrange("p j (m t) -> p m j t", t=PACK)[:, :, :, 2 * e : 2 * e + 2],
+            )
+
+        round_w1(nc.scalar.copy, 0, 0)
+        round_w1(nc.scalar.copy, 0, 1)
+        round_w1(nc.vector.tensor_copy, 1, 0)
+        round_w1(nc.scalar.copy, 1, 1)
         w1_codes = keep.tile([P, H], U32, name="w1_codes", align_bytes=64)
         w1_sc = keep.tile([P, H], U8, name="w1_sc", align_bytes=64)
         for t in range(2):

@@ -73,7 +73,7 @@ def tile_picked_inorm_relu_p_kernel(tc, x_words, x_scales, w1, w2, gamma, offs, 
         for u in range(2):
             nc.vector.tensor_copy(x_codes[u][:], table_words[:].indirect(offsets[:, 32 * u : 32 * (u + 1)]))
 
-        w1_bf = [keep.tile([P, 2, P * PACK], BF16, name=f"w1_bf{e}", align_bytes=64) for e in range(2)]
+        w1_bf = [keep.tile([P, 2, P * PACK], BF16, name=f"w1_bf{e}", tag=f"w1_bf{e}", align_bytes=64) for e in range(2)]
         def round_w1(engine_copy, a, e):
             engine_copy(
                 out=w1_bf[e][:].rearrange("p t (m j) -> p m j t", j=PACK)[:, :, 2 * a : 2 * a + 2, :],
@@ -86,7 +86,7 @@ def tile_picked_inorm_relu_p_kernel(tc, x_words, x_scales, w1, w2, gamma, offs, 
         round_w1(nc.scalar.copy, 1, 1)
         w1_codes = keep.tile([P, H], U32, name="w1_codes", align_bytes=64)
         w1_sc = keep.tile([P, H], U8, name="w1_sc", align_bytes=64)
-        for t in range(2):
+        for t in (1, 0):
             nc.vector.quantize_mx(
                 out=w1_codes[:, P * t : P * (t + 1)].bitcast(FP8X4), scales=w1_sc[:, P * t : P * (t + 1)],
                 in_=w1_bf[0][:, t, :],
@@ -109,7 +109,7 @@ def tile_picked_inorm_relu_p_kernel(tc, x_words, x_scales, w1, w2, gamma, offs, 
             )
 
         h = {}
-        for t, u in [(0, 0), (1, 0), (0, 1), (2, 0), (1, 1), (2, 1), (3, 0), (3, 1)]:
+        for t, u in [(1, 0), (0, 0), (0, 1), (2, 0), (1, 1), (2, 1), (3, 0), (3, 1)]:
             bank = psum.tile([P, HALF], F32, name=f"h{t}{u}", tag=f"bank{2 * t + u}")
             nc.tensor.matmul_mx(
                 out=bank[:],
@@ -127,6 +127,7 @@ def tile_picked_inorm_relu_p_kernel(tc, x_words, x_scales, w1, w2, gamma, offs, 
 
         z_rows = [keep.tile([P, PACK, QUARTER], BF16, name=f"z_rows{c}", align_bytes=64) for c in range(4)]
         affine = [keep.tile([P, 3], F32, name=f"affine{t}") for t in range(PACK)]
+        rstd = [keep.tile([P, 1], F32, name=f"rstd{t}") for t in range(PACK)]
         shrunk = {}
 
         def stats_vector(t, u):
@@ -148,13 +149,18 @@ def tile_picked_inorm_relu_p_kernel(tc, x_words, x_scales, w1, w2, gamma, offs, 
         def aggregate(t):
             tuples = stats[t][:, 3:15] if t in (1, 3) else stats[t][:, 0:9]
             nc.vector.bn_aggr(out=moments[t][:, 2:4], in_=tuples)
-            rstd = keep.tile([P, 1], F32, name=f"rstd{t}")
-            nc.scalar.activation(out=rstd[:], in_=moments[t][:, 3:4], func=ACT.Abs_reciprocal_sqrt, bias=EPS)
-            engine = nc.gpsimd if t == 0 else nc.vector
-            engine.tensor_scalar(
-                out=affine[t][:], in0=moments[t][:, 0:3], scalar1=neg_gamma[:, t : t + 1], scalar2=rstd[:],
+            nc.scalar.activation(out=rstd[t][:], in_=moments[t][:, 3:4], func=ACT.Abs_reciprocal_sqrt, bias=EPS)
+
+        def make_affine(t):
+            nc.vector.tensor_scalar(
+                out=affine[t][:], in0=moments[t][:, 0:3], scalar1=neg_gamma[:, t : t + 1], scalar2=rstd[t][:],
                 op0=ALU.mult, op1=ALU.mult,
             )
+
+        def make_affine_scalar(t):
+            gained = keep.tile([P, 3], F32, name=f"gained{t}")
+            nc.scalar.activation(out=gained[:], in_=moments[t][:, 0:3], func=ACT.Copy, scale=neg_gamma[:, t : t + 1])
+            nc.scalar.activation(out=affine[t][:], in_=gained[:], func=ACT.Copy, scale=rstd[t][:])
 
         def quarter_of(half_tile, c):
             return half_tile[:, QUARTER * (c % 2) : QUARTER * (c % 2 + 1)]
@@ -165,10 +171,16 @@ def tile_picked_inorm_relu_p_kernel(tc, x_words, x_scales, w1, w2, gamma, offs, 
                 scale=affine[t][:, 1:2], bias=affine[t][:, 2:3],
             )
 
-        def normalise_vector(t, c):
+        def normalise_gpsimd(t, c):
+            nc.gpsimd.tensor_scalar(
+                out=z_rows[c][:, t, :], in0=quarter_of(shrunk[t], c), scalar1=affine[t][:, 0:1],
+                scalar2=affine[t][:, 2:3], op0=ALU.mult, op1=ALU.add,
+            )
+
+        def normalise_vector(t, c, cols=slice(0, QUARTER)):
             source, col = (shrunk[t], 0) if t in shrunk else (h[t, 0], 1)
             nc.vector.tensor_scalar(
-                out=z_rows[c][:, t, :], in0=quarter_of(source, c), scalar1=affine[t][:, col : col + 1],
+                out=z_rows[c][:, t, cols], in0=quarter_of(source, c)[:, cols], scalar1=affine[t][:, col : col + 1],
                 scalar2=affine[t][:, 2:3], op0=ALU.mult, op1=ALU.add,
             )
 
@@ -176,33 +188,39 @@ def tile_picked_inorm_relu_p_kernel(tc, x_words, x_scales, w1, w2, gamma, offs, 
         stats_vector(1, 0)
         stats_vector(0, 1)
         aggregate(0)
+        make_affine_scalar(0)
         stats_vector(1, 1)
         aggregate(1)
+        make_affine_scalar(1)
         stats_scalar(2)
         stats_vector(2, 1)
         aggregate(2)
         stats_vector(3, 0)
         stats_vector(3, 1)
         aggregate(3)
-        w2_bf = keep.tile([P, N, PACK], BF16, name="w2_bf", tag="scratch0", align_bytes=64)
+        w2_bf = keep.tile([P, N, PACK], BF16, name="w2_bf", tag="w1_bf1", align_bytes=64)
         w2_cols = w2_raw[:].rearrange("p j n -> p n j")
-        for n0 in range(0, N, 64):
+        for n0 in range(0, N, P):
             nc.gpsimd.tensor_scalar(
-                out=w2_bf[:, n0 : n0 + 64, :], in0=w2_cols[:, n0 : n0 + 64, :],
+                out=w2_bf[:, n0 : n0 + P, :], in0=w2_cols[:, n0 : n0 + P, :],
                 scalar1=1.0, scalar2=0.0, op0=ALU.mult, op1=ALU.add,
             )
-        normalise_scalar(1, 0)
-        normalise_vector(0, 0)
-        normalise_vector(2, 0)
-        normalise_vector(3, 0)
-        for t in (1, 2, 3):
-            normalise_scalar(t, 1)
-        normalise_vector(0, 1)
-        for t in range(PACK):
-            normalise_scalar(t, 3)
-
         w2_codes = keep.tile([P, N], U32, name="w2_codes", align_bytes=64)
         w2_sc = keep.tile([P, N], U8, name="w2_sc", align_bytes=64)
+        normalise_gpsimd(0, 0)
+        normalise_gpsimd(0, 1)
+        nc.vector.quantize_mx(out=w2_codes[:].bitcast(FP8X4), scales=w2_sc[:], in_=w2_bf[:].rearrange("p n j -> p (n j)"))
+        make_affine(2)
+        make_affine(3)
+        normalise_scalar(1, 0)
+        normalise_vector(3, 0, slice(0, P))
+        normalise_vector(3, 0, slice(P, QUARTER))
+        normalise_vector(2, 0)
+        normalise_vector(2, 1)
+        normalise_vector(3, 1)
+        normalise_scalar(1, 1)
+        for t in range(PACK):
+            normalise_scalar(t, 3)
 
         pieces = [(c, lo, 128) for c in (0, 1, 3, 2) for lo in (0, 128)]
         z_codes = [
@@ -262,7 +280,6 @@ def tile_picked_inorm_relu_p_kernel(tc, x_words, x_scales, w1, w2, gamma, offs, 
                 engine_copy(out=res[:], in_=acc[:])
                 nc.sync.dma_start(out=out[P * m : P * (m + 1), col : col + w], in_=res[:])
 
-        nc.vector.quantize_mx(out=w2_codes[:].bitcast(FP8X4), scales=w2_sc[:], in_=w2_bf[:].rearrange("p n j -> p (n j)"))
         interleave_vector(0)
         interleave_vector(1)
         quantise(0)

@@ -171,12 +171,6 @@ def tile_picked_inorm_relu_p_kernel(tc, x_words, x_scales, w1, w2, gamma, offs, 
                 scale=affine[t][:, 1:2], bias=affine[t][:, 2:3],
             )
 
-        def normalise_gpsimd(t, c):
-            nc.gpsimd.tensor_scalar(
-                out=z_rows[c][:, t, :], in0=quarter_of(shrunk[t], c), scalar1=affine[t][:, 0:1],
-                scalar2=affine[t][:, 2:3], op0=ALU.mult, op1=ALU.add,
-            )
-
         def normalise_vector(t, c, cols=slice(0, QUARTER)):
             source, col = (shrunk[t], 0) if t in shrunk else (h[t, 0], 1)
             nc.vector.tensor_scalar(
@@ -207,8 +201,8 @@ def tile_picked_inorm_relu_p_kernel(tc, x_words, x_scales, w1, w2, gamma, offs, 
             )
         w2_codes = keep.tile([P, N], U32, name="w2_codes", align_bytes=64)
         w2_sc = keep.tile([P, N], U8, name="w2_sc", align_bytes=64)
-        normalise_gpsimd(0, 0)
-        normalise_gpsimd(0, 1)
+        normalise_vector(0, 0)
+        normalise_vector(0, 1)
         nc.vector.quantize_mx(out=w2_codes[:].bitcast(FP8X4), scales=w2_sc[:], in_=w2_bf[:].rearrange("p n j -> p (n j)"))
         make_affine(2)
         make_affine(3)

@@ -28,13 +28,13 @@ def tile_picked_inorm_relu_p_kernel(tc, x_words, x_scales, w1, w2, gamma, offs, 
     nc = tc.nc
     with ExitStack() as ctx:
         keep = ctx.enter_context(tc.tile_pool(name="keep", bufs=1))
+        reused = ctx.enter_context(tc.tile_pool(name="reused", bufs=1))
         psum = ctx.enter_context(tc.psum_pool(name="psum", bufs=1))
 
         offsets = keep.tile([P, S // 16], U16, name="offsets")
         table_words = keep.tile([P, T], U32, name="table_words", align_bytes=64)
-        table_scales = keep.tile([P, T], U8, name="table_scales", tag="scales_then_w2", align_bytes=64)
+        table_scales = reused.tile([P, T], U8, name="table_scales", offset=0)
         w1_raw = [keep.tile([P, 2, H], F32, name=f"w1_raw{a}") for a in range(2)]
-        gamma_sb = keep.tile([P, PACK], F32, name="gamma_sb")
 
         nc.vector.memset(table_scales[:].bitcast(I32), 0)
         words = x_words[0].rearrange("p n t -> p (n t)").bitcast(I32)
@@ -45,7 +45,6 @@ def tile_picked_inorm_relu_p_kernel(tc, x_words, x_scales, w1, w2, gamma, offs, 
         w1_rows = w1.rearrange("(p j) c -> p j c", j=PACK)
         for a in range(2):
             nc.sync.dma_start(out=w1_raw[a][:], in_=w1_rows[:, 2 * a : 2 * a + 2, :])
-        nc.sync.dma_start(out=gamma_sb[:], in_=gamma.rearrange("(p t) o -> p (t o)", t=PACK))
 
         warm_in = keep.tile([P, 1], F32, name="warm_in")
         warm_out = keep.tile([P, 1], F32, name="warm_out")
@@ -66,7 +65,9 @@ def tile_picked_inorm_relu_p_kernel(tc, x_words, x_scales, w1, w2, gamma, offs, 
         nc.vector.tensor_copy(picked_sc[:], table_scales[:].indirect(offsets[:]))
         for r in range(4):
             nc.sync.dma_start(out=x_sc[r:P:32, :].bitcast(I32), in_=picked_sc[8 * r : P : 32, :].bitcast(I32))
-        w2_raw = keep.tile([P, PACK, N], F32, name="w2_raw", tag="scales_then_w2", align_bytes=64)
+        gamma_sb = reused.tile([P, PACK], F32, name="gamma_sb", offset=0)
+        nc.sync.dma_start(out=gamma_sb[:], in_=gamma.rearrange("(p t) o -> p (t o)", t=PACK))
+        w2_raw = reused.tile([P, PACK, N], F32, name="w2_raw", offset=64)
         nc.sync.dma_start(out=w2_raw[:], in_=w2.rearrange("(p j) c -> p j c", j=PACK))
 
         x_codes = [keep.tile([P, HALF], U32, name=f"x_codes{u}", align_bytes=64) for u in range(2)]
@@ -97,13 +98,13 @@ def tile_picked_inorm_relu_p_kernel(tc, x_words, x_scales, w1, w2, gamma, offs, 
         )
 
         warm_bank = psum.tile([P, HALF], F32, name="warm_bank", tag="bank7")
-        for i in range(2):
+        for u in (0, 0, 1):
             nc.tensor.matmul_mx(
                 out=warm_bank[:],
                 lhsT=x_codes[0][:, 0:P].bitcast(FP8X4),
                 lhsT_scale=picked_sc[:, 0:P],
-                rhs=x_codes[0][:].bitcast(FP8X4),
-                rhs_scale=picked_sc[:, :HALF],
+                rhs=x_codes[u][:].bitcast(FP8X4),
+                rhs_scale=picked_sc[:, HALF * u : HALF * (u + 1)],
                 start=True,
                 stop=True,
             )
@@ -111,15 +112,16 @@ def tile_picked_inorm_relu_p_kernel(tc, x_words, x_scales, w1, w2, gamma, offs, 
         h = {}
         for t, u in [(1, 0), (0, 0), (0, 1), (2, 0), (1, 1), (2, 1), (3, 0), (3, 1)]:
             bank = psum.tile([P, HALF], F32, name=f"h{t}{u}", tag=f"bank{2 * t + u}")
-            nc.tensor.matmul_mx(
-                out=bank[:],
-                lhsT=w1_codes[:, P * t : P * (t + 1)].bitcast(FP8X4),
-                lhsT_scale=w1_sc[:, P * t : P * (t + 1)],
-                rhs=x_codes[u][:].bitcast(FP8X4),
-                rhs_scale=x_sc[:, HALF * u : HALF * (u + 1)],
-                start=True,
-                stop=True,
-            )
+            for lo in (0, QUARTER):
+                nc.tensor.matmul_mx(
+                    out=bank[:, lo : lo + QUARTER],
+                    lhsT=w1_codes[:, P * t : P * (t + 1)].bitcast(FP8X4),
+                    lhsT_scale=w1_sc[:, P * t : P * (t + 1)],
+                    rhs=x_codes[u][:, lo : lo + QUARTER].bitcast(FP8X4),
+                    rhs_scale=x_sc[:, HALF * u + lo : HALF * u + lo + QUARTER],
+                    start=True,
+                    stop=True,
+                )
             h[t, u] = bank
 
         neg_gamma = keep.tile([P, PACK], F32, name="neg_gamma")

@@ -20,7 +20,8 @@ P = 128
 PACK = 4
 HALF = 512
 QUARTER = 256
-FIRST_COLS = 1024
+FIRST_COLS = 640
+W1_SPLIT = 80
 SCALAR_STATS = (0, 2)
 
 
@@ -33,18 +34,20 @@ def tile_picked_inorm_relu_p_kernel(tc, x_words, x_scales, w1, w2, gamma, offs, 
 
         offsets = keep.tile([P, S // 16], U16, name="offsets")
         table_words = keep.tile([P, T], U32, name="table_words", align_bytes=64)
-        table_scales = reused.tile([P, T], U8, name="table_scales", offset=0)
-        w1_raw = [keep.tile([P, 2, H], F32, name=f"w1_raw{a}") for a in range(2)]
+        table_scales = reused.tile([P, T], U8, name="table_scales", offset=T)
+        w1_first = keep.tile([P, 2, H], F32, name="w1_first")
 
-        nc.vector.memset(table_scales[:].bitcast(I32), 0)
+        scale_words = table_scales[:].bitcast(I32)
+        nc.gpsimd.memset(scale_words[:, :512], 0)
+        nc.vector.memset(scale_words[:, 512:767], 0)
+        nc.vector.memset(scale_words[:, 767:], 0)
         words = x_words[0].rearrange("p n t -> p (n t)").bitcast(I32)
         nc.sync.dma_start(out=table_words[:, :FIRST_COLS].bitcast(I32), in_=words[:, :FIRST_COLS])
         nc.sync.dma_start(offsets[:], offs)
         nc.sync.dma_start(out=table_scales[0:P:8, :].bitcast(I32), in_=x_scales[0].bitcast(I32))
         nc.sync.dma_start(out=table_words[:, FIRST_COLS:].bitcast(I32), in_=words[:, FIRST_COLS:])
         w1_rows = w1.rearrange("(p j) c -> p j c", j=PACK)
-        for a in range(2):
-            nc.sync.dma_start(out=w1_raw[a][:], in_=w1_rows[:, 2 * a : 2 * a + 2, :])
+        nc.sync.dma_start(out=w1_first[:], in_=w1_rows[:, :2, :])
 
         warm_in = keep.tile([P, 1], F32, name="warm_in")
         warm_out = keep.tile([P, 1], F32, name="warm_out")
@@ -54,9 +57,9 @@ def tile_picked_inorm_relu_p_kernel(tc, x_words, x_scales, w1, w2, gamma, offs, 
         stats = [keep.tile([P, 15], F32, name=f"stats{t}") for t in range(PACK)]
         moments = [keep.tile([P, 4], F32, name=f"moments{t}") for t in range(PACK)]
         for t in range(PACK):
-            nc.vector.memset(moments[t][:, 0:1], -float(HALF))
             nc.vector.memset(moments[t][:, 1:2], -1.0)
         for t in SCALAR_STATS:
+            nc.vector.memset(moments[t][:, 0:1], -float(HALF))
             nc.vector.memset(stats[t][:, 0:1], float(HALF))
 
         picked_sc = keep.tile([P, S], U8, name="picked_sc", align_bytes=64)
@@ -65,7 +68,10 @@ def tile_picked_inorm_relu_p_kernel(tc, x_words, x_scales, w1, w2, gamma, offs, 
         nc.vector.tensor_copy(picked_sc[:], table_scales[:].indirect(offsets[:]))
         for r in range(4):
             nc.sync.dma_start(out=x_sc[r:P:32, :].bitcast(I32), in_=picked_sc[8 * r : P : 32, :].bitcast(I32))
-        gamma_sb = reused.tile([P, PACK], F32, name="gamma_sb", offset=0)
+        w1_second = reused.tile([P, 2, H], F32, name="w1_second", offset=2 * T - 64)
+        nc.sync.dma_start(out=w1_second[:], in_=w1_rows[:, 2:, :])
+        w1_raw = [w1_first, w1_second]
+        gamma_sb = reused.tile([P, PACK], F32, name="gamma_sb", offset=T + 128)
         nc.sync.dma_start(out=gamma_sb[:], in_=gamma.rearrange("(p t) o -> p (t o)", t=PACK))
         w2_raw = reused.tile([P, PACK, N], F32, name="w2_raw", offset=64)
         nc.sync.dma_start(out=w2_raw[:], in_=w2.rearrange("(p j) c -> p j c", j=PACK))
@@ -75,16 +81,17 @@ def tile_picked_inorm_relu_p_kernel(tc, x_words, x_scales, w1, w2, gamma, offs, 
             nc.vector.tensor_copy(x_codes[u][:], table_words[:].indirect(offsets[:, 32 * u : 32 * (u + 1)]))
 
         w1_bf = [keep.tile([P, 2, P * PACK], BF16, name=f"w1_bf{e}", tag=f"w1_bf{e}", align_bytes=64) for e in range(2)]
-        def round_w1(engine_copy, a, e):
+        def round_w1(engine_copy, a, e, cols=slice(0, P)):
             engine_copy(
-                out=w1_bf[e][:].rearrange("p t (m j) -> p m j t", j=PACK)[:, :, 2 * a : 2 * a + 2, :],
-                in_=w1_raw[a][:].rearrange("p j (m t) -> p m j t", t=PACK)[:, :, :, 2 * e : 2 * e + 2],
+                out=w1_bf[e][:].rearrange("p t (m j) -> p m j t", j=PACK)[:, cols, 2 * a : 2 * a + 2, :],
+                in_=w1_raw[a][:].rearrange("p j (m t) -> p m j t", t=PACK)[:, cols, :, 2 * e : 2 * e + 2],
             )
 
         round_w1(nc.scalar.copy, 0, 0)
         round_w1(nc.scalar.copy, 0, 1)
         round_w1(nc.vector.tensor_copy, 1, 0)
-        round_w1(nc.scalar.copy, 1, 1)
+        round_w1(nc.vector.tensor_copy, 1, 1, slice(0, W1_SPLIT))
+        round_w1(nc.scalar.copy, 1, 1, slice(W1_SPLIT, P))
         w1_codes = keep.tile([P, H], U32, name="w1_codes", align_bytes=64)
         w1_sc = keep.tile([P, H], U8, name="w1_sc", align_bytes=64)
         for t in (1, 0):
@@ -102,9 +109,9 @@ def tile_picked_inorm_relu_p_kernel(tc, x_words, x_scales, w1, w2, gamma, offs, 
             nc.tensor.matmul_mx(
                 out=warm_bank[:],
                 lhsT=x_codes[0][:, 0:P].bitcast(FP8X4),
-                lhsT_scale=picked_sc[:, 0:P],
+                lhsT_scale=x_sc[:, 0:P],
                 rhs=x_codes[u][:].bitcast(FP8X4),
-                rhs_scale=picked_sc[:, HALF * u : HALF * (u + 1)],
+                rhs_scale=x_sc[:, HALF * u : HALF * (u + 1)],
                 start=True,
                 stop=True,
             )
@@ -154,15 +161,17 @@ def tile_picked_inorm_relu_p_kernel(tc, x_words, x_scales, w1, w2, gamma, offs, 
             nc.scalar.activation(out=rstd[t][:], in_=moments[t][:, 3:4], func=ACT.Abs_reciprocal_sqrt, bias=EPS)
 
         def make_affine(t):
+            lo = 0 if t in SCALAR_STATS else 1
             nc.vector.tensor_scalar(
-                out=affine[t][:], in0=moments[t][:, 0:3], scalar1=neg_gamma[:, t : t + 1], scalar2=rstd[t][:],
+                out=affine[t][:, lo:3], in0=moments[t][:, lo:3], scalar1=neg_gamma[:, t : t + 1], scalar2=rstd[t][:],
                 op0=ALU.mult, op1=ALU.mult,
             )
 
         def make_affine_scalar(t):
-            gained = keep.tile([P, 3], F32, name=f"gained{t}")
-            nc.scalar.activation(out=gained[:], in_=moments[t][:, 0:3], func=ACT.Copy, scale=neg_gamma[:, t : t + 1])
-            nc.scalar.activation(out=affine[t][:], in_=gained[:], func=ACT.Copy, scale=rstd[t][:])
+            lo = 0 if t in SCALAR_STATS else 1
+            gained = keep.tile([P, 3 - lo], F32, name=f"gained{t}")
+            nc.scalar.activation(out=gained[:], in_=moments[t][:, lo:3], func=ACT.Copy, scale=neg_gamma[:, t : t + 1])
+            nc.scalar.activation(out=affine[t][:, lo:3], in_=gained[:], func=ACT.Copy, scale=rstd[t][:])
 
         def quarter_of(half_tile, c):
             return half_tile[:, QUARTER * (c % 2) : QUARTER * (c % 2 + 1)]

@@ -134,7 +134,10 @@ def tile_picked_inorm_relu_p_kernel(tc, x_words, x_scales, w1, w2, gamma, offs, 
         neg_gamma = keep.tile([P, PACK], F32, name="neg_gamma")
         nc.scalar.activation(out=neg_gamma[:], in_=gamma_sb[:], func=ACT.Copy, scale=-1.0)
 
-        z_rows = [keep.tile([P, PACK, QUARTER], BF16, name=f"z_rows{c}", align_bytes=64) for c in range(4)]
+        z_halves = [keep.tile([P, PACK * HALF], BF16, name=f"z_half{u}", align_bytes=64) for u in range(2)]
+        half_rows = [z_half[:].rearrange("p (t n) -> p t n", t=PACK) for z_half in z_halves]
+        late_rows = half_rows[1]
+        z_rows = [half_rows[c // 2][:, :, QUARTER * (c % 2) : QUARTER * (c % 2 + 1)] for c in range(4)]
         affine = [keep.tile([P, 3], F32, name=f"affine{t}") for t in range(PACK)]
         rstd = [keep.tile([P, 1], F32, name=f"rstd{t}") for t in range(PACK)]
         shrunk = {}
@@ -176,10 +179,21 @@ def tile_picked_inorm_relu_p_kernel(tc, x_words, x_scales, w1, w2, gamma, offs, 
         def quarter_of(half_tile, c):
             return half_tile[:, QUARTER * (c % 2) : QUARTER * (c % 2 + 1)]
 
-        def normalise_scalar(t, c):
+        def normalise_scalar(t, c, cols=slice(0, QUARTER)):
             nc.scalar.activation(
-                out=z_rows[c][:, t, :], in_=quarter_of(h[t, c // 2], c), func=ACT.Relu,
+                out=z_rows[c][:, t, cols], in_=quarter_of(h[t, c // 2], c)[:, cols], func=ACT.Relu,
                 scale=affine[t][:, 1:2], bias=affine[t][:, 2:3],
+            )
+
+        def normalise_bank(t):
+            nc.scalar.activation(
+                out=late_rows[:, t, :], in_=h[t, 1][:], func=ACT.Relu, scale=affine[t][:, 1:2], bias=affine[t][:, 2:3]
+            )
+
+        def normalise_copy(t):
+            nc.vector.tensor_scalar(
+                out=half_rows[0][:, t, :], in0=shrunk[t][:], scalar1=affine[t][:, 0:1], scalar2=affine[t][:, 2:3],
+                op0=ALU.mult, op1=ALU.add,
             )
 
         def normalise_vector(t, c, cols=slice(0, QUARTER)):
@@ -212,20 +226,20 @@ def tile_picked_inorm_relu_p_kernel(tc, x_words, x_scales, w1, w2, gamma, offs, 
             )
         w2_codes = keep.tile([P, N], U32, name="w2_codes", align_bytes=64)
         w2_sc = keep.tile([P, N], U8, name="w2_sc", align_bytes=64)
-        normalise_vector(0, 0)
-        normalise_vector(0, 1)
+        normalise_copy(0)
         nc.vector.quantize_mx(out=w2_codes[:].bitcast(FP8X4), scales=w2_sc[:], in_=w2_bf[:].rearrange("p n j -> p (n j)"))
         make_affine(2)
         make_affine(3)
         normalise_scalar(1, 0)
         normalise_vector(3, 0, slice(0, P))
         normalise_vector(3, 0, slice(P, QUARTER))
-        normalise_vector(2, 0)
-        normalise_vector(2, 1)
-        normalise_vector(3, 1)
+        normalise_copy(2)
+        normalise_vector(3, 1, slice(0, P))
+        normalise_scalar(3, 1, slice(P, QUARTER))
         normalise_scalar(1, 1)
-        for t in range(PACK):
-            normalise_scalar(t, 3)
+        for t in range(PACK - 1):
+            normalise_bank(t)
+        normalise_scalar(3, 3)
 
         pieces = [(c, lo, 128) for c in (0, 1, 3, 2) for lo in (0, 128)]
         z_codes = [
@@ -295,8 +309,7 @@ def tile_picked_inorm_relu_p_kernel(tc, x_words, x_scales, w1, w2, gamma, offs, 
         interleave_vector(3)
         quantise(2)
         second_layer(2, 2, nc.scalar.copy)
-        for t in range(PACK):
-            normalise_scalar(t, 2)
+        normalise_scalar(3, 2)
         interleave_scalar(4)
         interleave_vector(5)
         quantise(3)
@@ -308,6 +321,6 @@ def tile_picked_inorm_relu_p_kernel(tc, x_words, x_scales, w1, w2, gamma, offs, 
         second_layer(4, 4, nc.scalar.copy)
         interleave_vector(7)
         quantise(6)
-        second_layer(6, 1, nc.scalar.copy)
         quantise(7)
+        second_layer(6, 1, nc.vector.tensor_copy)
         shared_second_layer(7, (3, 5))

@@ -19,10 +19,11 @@ ACT = mybir.ActivationFunctionType
 P = 128
 PACK = 4
 HALF = 512
-QUARTER = 256
+PIECE = 128
 FIRST_COLS = 640
 W1_SPLIT = 80
-SCALAR_STATS = (0, 2)
+COPIED = (0, 2)
+WARM_COLS = 32
 
 
 def tile_picked_inorm_relu_p_kernel(tc, x_words, x_scales, w1, w2, gamma, offs, out):
@@ -54,11 +55,11 @@ def tile_picked_inorm_relu_p_kernel(tc, x_words, x_scales, w1, w2, gamma, offs, 
         nc.gpsimd.memset(warm_in[:], 1.0)
         nc.scalar.activation(out=warm_out[:], in_=warm_in[:], func=ACT.Abs_reciprocal_sqrt)
 
-        stats = [keep.tile([P, 15], F32, name=f"stats{t}") for t in range(PACK)]
+        stats = [keep.tile([P, 12], F32, name=f"stats{t}") for t in range(PACK)]
         moments = [keep.tile([P, 4], F32, name=f"moments{t}") for t in range(PACK)]
         for t in range(PACK):
             nc.vector.memset(moments[t][:, 1:2], -1.0)
-        for t in SCALAR_STATS:
+        for t in COPIED:
             nc.vector.memset(moments[t][:, 0:1], -float(HALF))
             nc.vector.memset(stats[t][:, 0:1], float(HALF))
 
@@ -81,6 +82,7 @@ def tile_picked_inorm_relu_p_kernel(tc, x_words, x_scales, w1, w2, gamma, offs, 
             nc.vector.tensor_copy(x_codes[u][:], table_words[:].indirect(offsets[:, 32 * u : 32 * (u + 1)]))
 
         w1_bf = [keep.tile([P, 2, P * PACK], BF16, name=f"w1_bf{e}", tag=f"w1_bf{e}", align_bytes=64) for e in range(2)]
+
         def round_w1(engine_copy, a, e, cols=slice(0, P)):
             engine_copy(
                 out=w1_bf[e][:].rearrange("p t (m j) -> p m j t", j=PACK)[:, cols, 2 * a : 2 * a + 2, :],
@@ -107,9 +109,9 @@ def tile_picked_inorm_relu_p_kernel(tc, x_words, x_scales, w1, w2, gamma, offs, 
         warm_bank = psum.tile([P, HALF], F32, name="warm_bank", tag="bank7")
         for u in (0, 0, 1):
             nc.tensor.matmul_mx(
-                out=warm_bank[:],
-                lhsT=x_codes[0][:, 0:P].bitcast(FP8X4),
-                lhsT_scale=x_sc[:, 0:P],
+                out=warm_bank[0:WARM_COLS, :],
+                lhsT=x_codes[0][:, 0:WARM_COLS].bitcast(FP8X4),
+                lhsT_scale=x_sc[:, 0:WARM_COLS],
                 rhs=x_codes[u][:].bitcast(FP8X4),
                 rhs_scale=x_sc[:, HALF * u : HALF * (u + 1)],
                 start=True,
@@ -117,106 +119,77 @@ def tile_picked_inorm_relu_p_kernel(tc, x_words, x_scales, w1, w2, gamma, offs, 
             )
 
         h = {}
-        for t, u in [(1, 0), (0, 0), (0, 1), (2, 0), (1, 1), (2, 1), (3, 0), (3, 1)]:
+        for t, u in [(1, 0), (0, 0), (1, 1), (2, 0), (0, 1), (2, 1), (3, 0), (3, 1)]:
             bank = psum.tile([P, HALF], F32, name=f"h{t}{u}", tag=f"bank{2 * t + u}")
-            for lo in (0, QUARTER):
-                nc.tensor.matmul_mx(
-                    out=bank[:, lo : lo + QUARTER],
-                    lhsT=w1_codes[:, P * t : P * (t + 1)].bitcast(FP8X4),
-                    lhsT_scale=w1_sc[:, P * t : P * (t + 1)],
-                    rhs=x_codes[u][:, lo : lo + QUARTER].bitcast(FP8X4),
-                    rhs_scale=x_sc[:, HALF * u + lo : HALF * u + lo + QUARTER],
-                    start=True,
-                    stop=True,
-                )
+            nc.tensor.matmul_mx(
+                out=bank[:],
+                lhsT=w1_codes[:, P * t : P * (t + 1)].bitcast(FP8X4),
+                lhsT_scale=w1_sc[:, P * t : P * (t + 1)],
+                rhs=x_codes[u][:].bitcast(FP8X4),
+                rhs_scale=x_sc[:, HALF * u : HALF * (u + 1)],
+                start=True,
+                stop=True,
+            )
             h[t, u] = bank
 
         neg_gamma = keep.tile([P, PACK], F32, name="neg_gamma")
         nc.scalar.activation(out=neg_gamma[:], in_=gamma_sb[:], func=ACT.Copy, scale=-1.0)
 
         z_halves = [keep.tile([P, PACK * HALF], BF16, name=f"z_half{u}", align_bytes=64) for u in range(2)]
-        half_rows = [z_half[:].rearrange("p (t n) -> p t n", t=PACK) for z_half in z_halves]
-        late_rows = half_rows[1]
-        z_rows = [half_rows[c // 2][:, :, QUARTER * (c % 2) : QUARTER * (c % 2 + 1)] for c in range(4)]
+        z_rows = [z_half[:].rearrange("p (t n) -> p t n", t=PACK) for z_half in z_halves]
         affine = [keep.tile([P, 3], F32, name=f"affine{t}") for t in range(PACK)]
         rstd = [keep.tile([P, 1], F32, name=f"rstd{t}") for t in range(PACK)]
-        shrunk = {}
+        shrunk = {t: keep.tile([P, HALF], F32, name=f"shrunk{t}") for t in COPIED}
 
         def stats_vector(t, u):
-            lo = 3 + 6 * u if t in (1, 3) else 3
+            lo = 3 if t in COPIED else 6 * u
             nc.vector.bn_stats(out=stats[t][:, lo : lo + 6], in_=h[t, u][:])
 
-        def stats_scalar(t):
-            part = keep.tile([P, HALF], F32, name=f"shrunk{t}")
+        def sum_scalar(t):
             nc.scalar.activation(
-                out=part[:], in_=h[t, 0][:], func=ACT.Copy, scale=1.0 / HALF, accum_out=stats[t][:, 1:2]
+                out=shrunk[t][:], in_=h[t, 0][:], func=ACT.Copy, scale=1.0 / HALF, accum_out=stats[t][:, 1:2]
             )
-            squares = keep.tile([P, HALF], BF16, name=f"squares{t}", tag=f"scratch{t}", align_bytes=64)
+
+        def squares_scalar(t):
+            squares = keep.tile([P, HALF], BF16, name=f"squares{t}")
             nc.scalar.activation(
                 out=squares[:], in_=h[t, 0][:], func=ACT.Square, scale=-1.0, bias=stats[t][:, 1:2],
                 accum_out=stats[t][:, 2:3],
             )
-            shrunk[t] = part
 
         def aggregate(t):
-            tuples = stats[t][:, 3:15] if t in (1, 3) else stats[t][:, 0:9]
+            tuples = stats[t][:, 0:9] if t in COPIED else stats[t][:]
             nc.vector.bn_aggr(out=moments[t][:, 2:4], in_=tuples)
+
+        def root(t):
             nc.scalar.activation(out=rstd[t][:], in_=moments[t][:, 3:4], func=ACT.Abs_reciprocal_sqrt, bias=EPS)
 
-        def make_affine(t):
-            lo = 0 if t in SCALAR_STATS else 1
+        def affine_vector(t):
+            lo = 0 if t in COPIED else 1
             nc.vector.tensor_scalar(
                 out=affine[t][:, lo:3], in0=moments[t][:, lo:3], scalar1=neg_gamma[:, t : t + 1], scalar2=rstd[t][:],
                 op0=ALU.mult, op1=ALU.mult,
             )
 
-        def make_affine_scalar(t):
-            lo = 0 if t in SCALAR_STATS else 1
+        def affine_scalar(t):
+            lo = 0 if t in COPIED else 1
             gained = keep.tile([P, 3 - lo], F32, name=f"gained{t}")
             nc.scalar.activation(out=gained[:], in_=moments[t][:, lo:3], func=ACT.Copy, scale=neg_gamma[:, t : t + 1])
             nc.scalar.activation(out=affine[t][:, lo:3], in_=gained[:], func=ACT.Copy, scale=rstd[t][:])
 
-        def quarter_of(half_tile, c):
-            return half_tile[:, QUARTER * (c % 2) : QUARTER * (c % 2 + 1)]
-
-        def normalise_scalar(t, c, cols=slice(0, QUARTER)):
+        def normalise_scalar(t, u, cols=slice(0, HALF)):
             nc.scalar.activation(
-                out=z_rows[c][:, t, cols], in_=quarter_of(h[t, c // 2], c)[:, cols], func=ACT.Relu,
+                out=z_rows[u][:, t, cols], in_=h[t, u][:, cols], func=ACT.Relu,
                 scale=affine[t][:, 1:2], bias=affine[t][:, 2:3],
             )
 
-        def normalise_bank(t):
-            nc.scalar.activation(
-                out=late_rows[:, t, :], in_=h[t, 1][:], func=ACT.Relu, scale=affine[t][:, 1:2], bias=affine[t][:, 2:3]
-            )
-
-        def normalise_copy(t):
+        def normalise_vector(t, u, cols=slice(0, HALF)):
+            source, col = (shrunk[t], 0) if t in COPIED and u == 0 else (h[t, u], 1)
             nc.vector.tensor_scalar(
-                out=half_rows[0][:, t, :], in0=shrunk[t][:], scalar1=affine[t][:, 0:1], scalar2=affine[t][:, 2:3],
-                op0=ALU.mult, op1=ALU.add,
-            )
-
-        def normalise_vector(t, c, cols=slice(0, QUARTER)):
-            source, col = (shrunk[t], 0) if t in shrunk else (h[t, 0], 1)
-            nc.vector.tensor_scalar(
-                out=z_rows[c][:, t, cols], in0=quarter_of(source, c)[:, cols], scalar1=affine[t][:, col : col + 1],
+                out=z_rows[u][:, t, cols], in0=source[:, cols], scalar1=affine[t][:, col : col + 1],
                 scalar2=affine[t][:, 2:3], op0=ALU.mult, op1=ALU.add,
             )
 
-        stats_scalar(0)
-        stats_vector(1, 0)
-        stats_vector(0, 1)
-        aggregate(0)
-        make_affine_scalar(0)
-        stats_vector(1, 1)
-        aggregate(1)
-        make_affine_scalar(1)
-        stats_scalar(2)
-        stats_vector(2, 1)
-        aggregate(2)
-        stats_vector(3, 0)
-        stats_vector(3, 1)
-        aggregate(3)
         w2_bf = keep.tile([P, N, PACK], BF16, name="w2_bf", tag="w1_bf1", align_bytes=64)
         w2_cols = w2_raw[:].rearrange("p j n -> p n j")
         for n0 in range(0, N, P):
@@ -226,35 +199,50 @@ def tile_picked_inorm_relu_p_kernel(tc, x_words, x_scales, w1, w2, gamma, offs, 
             )
         w2_codes = keep.tile([P, N], U32, name="w2_codes", align_bytes=64)
         w2_sc = keep.tile([P, N], U8, name="w2_sc", align_bytes=64)
-        normalise_copy(0)
-        nc.vector.quantize_mx(out=w2_codes[:].bitcast(FP8X4), scales=w2_sc[:], in_=w2_bf[:].rearrange("p n j -> p (n j)"))
-        make_affine(2)
-        make_affine(3)
-        normalise_scalar(1, 0)
-        normalise_vector(3, 0, slice(0, P))
-        normalise_vector(3, 0, slice(P, QUARTER))
-        normalise_copy(2)
-        normalise_vector(3, 1, slice(0, P))
-        normalise_scalar(3, 1, slice(P, QUARTER))
-        normalise_scalar(1, 1)
-        for t in range(PACK - 1):
-            normalise_bank(t)
-        normalise_scalar(3, 3)
 
-        pieces = [(c, lo, 128) for c in (0, 1, 3, 2) for lo in (0, 128)]
-        z_codes = [
-            keep.tile([P, w], U32, name=f"z_codes{i}", tag=f"z_codes{i}", align_bytes=64)
-            for i, (c, lo, w) in enumerate(pieces)
-        ]
-        z_bf = [
-            keep.tile([P, w * PACK], BF16, name=f"z_bf{i}", tag="z_codes0" if i == 4 else f"z_bf{i}", align_bytes=64)
-            for i, (c, lo, w) in enumerate(pieces)
-        ]
-        z_sc = [keep.tile([P, w], U8, name=f"z_sc{i}", align_bytes=64) for i, (c, lo, w) in enumerate(pieces)]
+        sum_scalar(0)
+        sum_scalar(2)
+        squares_scalar(0)
+        stats_vector(1, 0)
+        stats_vector(1, 1)
+        aggregate(1)
+        root(1)
+        squares_scalar(2)
+        affine_scalar(1)
+        stats_vector(0, 1)
+        aggregate(0)
+        root(0)
+        affine_scalar(0)
+        stats_vector(2, 1)
+        aggregate(2)
+        root(2)
+        stats_vector(3, 0)
+        stats_vector(3, 1)
+        aggregate(3)
+        root(3)
+        normalise_vector(0, 0)
+        nc.vector.quantize_mx(out=w2_codes[:].bitcast(FP8X4), scales=w2_sc[:], in_=w2_bf[:].rearrange("p n j -> p (n j)"))
+        affine_vector(2)
+        affine_vector(3)
+        normalise_scalar(1, 0, slice(0, 2 * PIECE))
+        normalise_vector(3, 0, slice(0, PIECE))
+        normalise_vector(3, 0, slice(PIECE, 2 * PIECE))
+        normalise_vector(2, 0)
+        normalise_vector(3, 0, slice(2 * PIECE, 3 * PIECE))
+        normalise_scalar(3, 0, slice(3 * PIECE, HALF))
+        normalise_scalar(1, 0, slice(2 * PIECE, HALF))
+        for t in range(PACK - 1):
+            normalise_scalar(t, 1)
+        normalise_scalar(3, 1, slice(0, 2 * PIECE))
+
+        pieces = range(S // PIECE)
+        z_codes = [keep.tile([P, PIECE], U32, name=f"z_codes{i}", align_bytes=64) for i in pieces]
+        z_bf = [keep.tile([P, PIECE * PACK], BF16, name=f"z_bf{i}", align_bytes=64) for i in pieces]
+        z_sc = [keep.tile([P, PIECE], U8, name=f"z_sc{i}", align_bytes=64) for i in pieces]
 
         def rows_of(i):
-            c, lo, w = pieces[i]
-            return z_rows[c][:, :, lo : lo + w].rearrange("p t (g i) -> p g t i", i=4)
+            u, lo = divmod(PIECE * i, HALF)
+            return z_rows[u][:, :, lo : lo + PIECE].rearrange("p t (g i) -> p g t i", i=4)
 
         def words_of(i):
             return z_bf[i][:].rearrange("p (g i t) -> p g t i", i=4, t=PACK)
@@ -280,24 +268,22 @@ def tile_picked_inorm_relu_p_kernel(tc, x_words, x_scales, w1, w2, gamma, offs, 
             )
 
         def second_layer(i, bank, engine_copy):
-            c, lo, w = pieces[i]
-            col = QUARTER * c + lo
-            acc = psum.tile([P, 2, w], F32, name=f"acc{i}", tag=f"bank{bank}")
+            col = PIECE * i
+            acc = psum.tile([P, 2, PIECE], F32, name=f"acc{i}", tag=f"bank{bank}")
             for m in range(2):
                 product(i, m, acc[:, m, :])
-            res = keep.tile([P, 2, w], F32, name=f"res{i}")
+            res = keep.tile([P, 2, PIECE], F32, name=f"res{i}")
             engine_copy(out=res[:], in_=acc[:])
-            nc.sync.dma_start(out=out[:, col : col + w].rearrange("(m p) n -> p m n", p=P), in_=res[:])
+            nc.sync.dma_start(out=out[:, col : col + PIECE].rearrange("(m p) n -> p m n", p=P), in_=res[:])
 
         def shared_second_layer(i, banks):
-            c, lo, w = pieces[i]
-            col = QUARTER * c + lo
+            col = PIECE * i
             for m, engine_copy in enumerate((nc.scalar.copy, nc.vector.tensor_copy)):
-                acc = psum.tile([P, w], F32, name=f"acc{i}{m}", tag=f"bank{banks[m]}")
+                acc = psum.tile([P, PIECE], F32, name=f"acc{i}{m}", tag=f"bank{banks[m]}")
                 product(i, m, acc[:])
-                res = keep.tile([P, w], F32, name=f"res{i}{m}")
+                res = keep.tile([P, PIECE], F32, name=f"res{i}{m}")
                 engine_copy(out=res[:], in_=acc[:])
-                nc.sync.dma_start(out=out[P * m : P * (m + 1), col : col + w], in_=res[:])
+                nc.sync.dma_start(out=out[P * m : P * (m + 1), col : col + PIECE], in_=res[:])
 
         interleave_vector(0)
         interleave_vector(1)
@@ -309,7 +295,7 @@ def tile_picked_inorm_relu_p_kernel(tc, x_words, x_scales, w1, w2, gamma, offs, 
         interleave_vector(3)
         quantise(2)
         second_layer(2, 2, nc.scalar.copy)
-        normalise_scalar(3, 2)
+        normalise_scalar(3, 1, slice(2 * PIECE, HALF))
         interleave_scalar(4)
         interleave_vector(5)
         quantise(3)

@@ -267,31 +267,33 @@ def tile_picked_inorm_relu_p_kernel(tc, x_words, x_scales, w1, w2, gamma, offs, 
                 stop=True,
             )
 
+        res = keep.tile([P, 2, S], F32, name="res")
+
         def second_layer(i, bank, engine_copy):
-            col = PIECE * i
             acc = psum.tile([P, 2, PIECE], F32, name=f"acc{i}", tag=f"bank{bank}")
             for m in range(2):
                 product(i, m, acc[:, m, :])
-            res = keep.tile([P, 2, PIECE], F32, name=f"res{i}")
-            engine_copy(out=res[:], in_=acc[:])
-            nc.sync.dma_start(out=out[:, col : col + PIECE].rearrange("(m p) n -> p m n", p=P), in_=res[:])
+            engine_copy(out=res[:, :, PIECE * i : PIECE * (i + 1)], in_=acc[:])
 
         def shared_second_layer(i, banks):
-            col = PIECE * i
             for m, engine_copy in enumerate((nc.scalar.copy, nc.vector.tensor_copy)):
                 acc = psum.tile([P, PIECE], F32, name=f"acc{i}{m}", tag=f"bank{banks[m]}")
                 product(i, m, acc[:])
-                res = keep.tile([P, PIECE], F32, name=f"res{i}{m}")
-                engine_copy(out=res[:], in_=acc[:])
-                nc.sync.dma_start(out=out[P * m : P * (m + 1), col : col + PIECE], in_=res[:])
+                engine_copy(out=res[:, m, PIECE * i : PIECE * (i + 1)], in_=acc[:])
+
+        def store(first, count, halves=slice(0, 2)):
+            cols = slice(PIECE * first, PIECE * (first + count))
+            nc.sync.dma_start(out=out.rearrange("(m p) n -> p m n", p=P)[:, halves, cols], in_=res[:, halves, cols])
 
         interleave_vector(0)
         interleave_vector(1)
         quantise(0)
         second_layer(0, 0, nc.scalar.copy)
+        store(0, 1)
         interleave_vector(2)
         quantise(1)
         second_layer(1, 4, nc.scalar.copy)
+        store(1, 1)
         interleave_vector(3)
         quantise(2)
         second_layer(2, 2, nc.scalar.copy)
@@ -300,13 +302,17 @@ def tile_picked_inorm_relu_p_kernel(tc, x_words, x_scales, w1, w2, gamma, offs, 
         interleave_vector(5)
         quantise(3)
         second_layer(3, 6, nc.scalar.copy)
+        store(2, 2)
         interleave_vector(6)
         quantise(5)
         second_layer(5, 0, nc.scalar.copy)
         quantise(4)
         second_layer(4, 4, nc.scalar.copy)
+        store(4, 2)
         interleave_vector(7)
         quantise(6)
         quantise(7)
         second_layer(6, 1, nc.vector.tensor_copy)
         shared_second_layer(7, (3, 5))
+        for m in range(2):
+            store(6, 2, slice(m, m + 1))

@@ -281,9 +281,9 @@ def tile_picked_inorm_relu_p_kernel(tc, x_words, x_scales, w1, w2, gamma, offs, 
                 product(i, m, acc[:])
                 engine_copy(out=res[:, m, PIECE * i : PIECE * (i + 1)], in_=acc[:])
 
-        def store(first, count, halves=slice(0, 2)):
+        def store(first, count):
             cols = slice(PIECE * first, PIECE * (first + count))
-            nc.sync.dma_start(out=out.rearrange("(m p) n -> p m n", p=P)[:, halves, cols], in_=res[:, halves, cols])
+            nc.sync.dma_start(out=out.rearrange("(m p) n -> p m n", p=P)[:, :, cols], in_=res[:, :, cols])
 
         interleave_vector(0)
         interleave_vector(1)
@@ -314,5 +314,4 @@ def tile_picked_inorm_relu_p_kernel(tc, x_words, x_scales, w1, w2, gamma, offs, 
         quantise(7)
         second_layer(6, 1, nc.vector.tensor_copy)
         shared_second_layer(7, (3, 5))
-        for m in range(2):
-            store(6, 2, slice(m, m + 1))
+        store(6, 2)

@@ -20,6 +20,8 @@ P = 128
 PACK = 4
 HALF = 512
 PIECE = 128
+QUARTER = 256
+LAST = 3
 FIRST_COLS = 640
 W1_SPLIT = 80
 COPIED = (0, 2)
@@ -119,18 +121,26 @@ def tile_picked_inorm_relu_p_kernel(tc, x_words, x_scales, w1, w2, gamma, offs, 
             )
 
         h = {}
-        for t, u in [(1, 0), (0, 0), (1, 1), (2, 0), (0, 1), (2, 1), (3, 0), (3, 1)]:
-            bank = psum.tile([P, HALF], F32, name=f"h{t}{u}", tag=f"bank{2 * t + u}")
-            nc.tensor.matmul_mx(
-                out=bank[:],
-                lhsT=w1_codes[:, P * t : P * (t + 1)].bitcast(FP8X4),
-                lhsT_scale=w1_sc[:, P * t : P * (t + 1)],
-                rhs=x_codes[u][:].bitcast(FP8X4),
-                rhs_scale=x_sc[:, HALF * u : HALF * (u + 1)],
-                start=True,
-                stop=True,
-            )
-            h[t, u] = bank
+        for t, b in [(1, 0), (0, 0), (1, 1), (2, 0), (0, 1), (2, 1), (3, 0), (3, 1)]:
+            bank = psum.tile([P, HALF], F32, name=f"h{t}{b}", tag=f"bank{2 * t + b}")
+            parts = [(b, 0, HALF, 0)] if t < LAST else [(u, QUARTER * b, QUARTER, QUARTER * u) for u in range(2)]
+            for u, lo, width, place in parts:
+                nc.tensor.matmul_mx(
+                    out=bank[:, place : place + width],
+                    lhsT=w1_codes[:, P * t : P * (t + 1)].bitcast(FP8X4),
+                    lhsT_scale=w1_sc[:, P * t : P * (t + 1)],
+                    rhs=x_codes[u][:, lo : lo + width].bitcast(FP8X4),
+                    rhs_scale=x_sc[:, HALF * u + lo : HALF * u + lo + width],
+                    start=True,
+                    stop=True,
+                )
+            h[t, b] = bank
+
+        def h_of(t, u, cols):
+            if t < LAST:
+                return h[t, u][:, cols]
+            b, lo = divmod(cols.start, QUARTER)
+            return h[t, b][:, QUARTER * u + lo : QUARTER * u + lo + cols.stop - cols.start]
 
         neg_gamma = keep.tile([P, PACK], F32, name="neg_gamma")
         nc.scalar.activation(out=neg_gamma[:], in_=gamma_sb[:], func=ACT.Copy, scale=-1.0)
@@ -179,14 +189,14 @@ def tile_picked_inorm_relu_p_kernel(tc, x_words, x_scales, w1, w2, gamma, offs, 
 
         def normalise_scalar(t, u, cols=slice(0, HALF)):
             nc.scalar.activation(
-                out=z_rows[u][:, t, cols], in_=h[t, u][:, cols], func=ACT.Relu,
+                out=z_rows[u][:, t, cols], in_=h_of(t, u, cols), func=ACT.Relu,
                 scale=affine[t][:, 1:2], bias=affine[t][:, 2:3],
             )
 
         def normalise_vector(t, u, cols=slice(0, HALF)):
-            source, col = (shrunk[t], 0) if t in COPIED and u == 0 else (h[t, u], 1)
+            source, col = (shrunk[t][:, cols], 0) if t in COPIED and u == 0 else (h_of(t, u, cols), 1)
             nc.vector.tensor_scalar(
-                out=z_rows[u][:, t, cols], in0=source[:, cols], scalar1=affine[t][:, col : col + 1],
+                out=z_rows[u][:, t, cols], in0=source, scalar1=affine[t][:, col : col + 1],
                 scalar2=affine[t][:, 2:3], op0=ALU.mult, op1=ALU.add,
             )
 
@@ -225,11 +235,10 @@ def tile_picked_inorm_relu_p_kernel(tc, x_words, x_scales, w1, w2, gamma, offs, 
         affine_vector(2)
         affine_vector(3)
         normalise_scalar(1, 0, slice(0, 2 * PIECE))
+        normalise_vector(2, 0)
         normalise_vector(3, 0, slice(0, PIECE))
         normalise_vector(3, 0, slice(PIECE, 2 * PIECE))
-        normalise_vector(2, 0)
-        normalise_vector(3, 0, slice(2 * PIECE, 3 * PIECE))
-        normalise_scalar(3, 0, slice(3 * PIECE, HALF))
+        normalise_scalar(3, 0, slice(2 * PIECE, HALF))
         normalise_scalar(1, 0, slice(2 * PIECE, HALF))
         for t in range(PACK - 1):
             normalise_scalar(t, 1)
@@ -306,10 +315,10 @@ def tile_picked_inorm_relu_p_kernel(tc, x_words, x_scales, w1, w2, gamma, offs, 
         interleave_vector(6)
         quantise(5)
         second_layer(5, 0, nc.scalar.copy)
+        interleave_vector(7)
         quantise(4)
         second_layer(4, 4, nc.scalar.copy)
         store(4, 2)
-        interleave_vector(7)
         quantise(6)
         quantise(7)
         second_layer(6, 1, nc.vector.tensor_copy)

@@ -109,13 +109,13 @@ def tile_picked_inorm_relu_p_kernel(tc, x_words, x_scales, w1, w2, gamma, offs, 
         )
 
         warm_bank = psum.tile([P, HALF], F32, name="warm_bank", tag="bank7")
-        for u in (0, 0, 1):
+        for u in (0, 0, 1, 1):
             nc.tensor.matmul_mx(
                 out=warm_bank[0:WARM_COLS, :],
                 lhsT=x_codes[0][:, 0:WARM_COLS].bitcast(FP8X4),
-                lhsT_scale=x_sc[:, 0:WARM_COLS],
+                lhsT_scale=picked_sc[:, 0:WARM_COLS],
                 rhs=x_codes[u][:].bitcast(FP8X4),
-                rhs_scale=x_sc[:, HALF * u : HALF * (u + 1)],
+                rhs_scale=picked_sc[:, HALF * u : HALF * (u + 1)],
                 start=True,
                 stop=True,
             )

@@ -51,6 +51,8 @@ def tile_picked_inorm_relu_p_kernel(tc, x_words, x_scales, w1, w2, gamma, offs, 
         nc.sync.dma_start(out=table_words[:, FIRST_COLS:].bitcast(I32), in_=words[:, FIRST_COLS:])
         w1_rows = w1.rearrange("(p j) c -> p j c", j=PACK)
         nc.sync.dma_start(out=w1_first[:], in_=w1_rows[:, :2, :])
+        w1_second = keep.tile([P, 2, H], F32, name="w1_second")
+        nc.sync.dma_start(out=w1_second[:], in_=w1_rows[:, 2:, :])
 
         warm_in = keep.tile([P, 1], F32, name="warm_in")
         warm_out = keep.tile([P, 1], F32, name="warm_out")
@@ -71,8 +73,6 @@ def tile_picked_inorm_relu_p_kernel(tc, x_words, x_scales, w1, w2, gamma, offs, 
         nc.vector.tensor_copy(picked_sc[:], table_scales[:].indirect(offsets[:]))
         for r in range(4):
             nc.sync.dma_start(out=x_sc[r:P:32, :].bitcast(I32), in_=picked_sc[8 * r : P : 32, :].bitcast(I32))
-        w1_second = reused.tile([P, 2, H], F32, name="w1_second", offset=2 * T - 64)
-        nc.sync.dma_start(out=w1_second[:], in_=w1_rows[:, 2:, :])
         w1_raw = [w1_first, w1_second]
         gamma_sb = reused.tile([P, PACK], F32, name="gamma_sb", offset=T + 128)
         nc.sync.dma_start(out=gamma_sb[:], in_=gamma.rearrange("(p t) o -> p (t o)", t=PACK))
@@ -80,8 +80,9 @@ def tile_picked_inorm_relu_p_kernel(tc, x_words, x_scales, w1, w2, gamma, offs, 
         nc.sync.dma_start(out=w2_raw[:], in_=w2.rearrange("(p j) c -> p j c", j=PACK))
 
         x_codes = [keep.tile([P, HALF], U32, name=f"x_codes{u}", align_bytes=64) for u in range(2)]
-        for u in range(2):
-            nc.vector.tensor_copy(x_codes[u][:], table_words[:].indirect(offsets[:, 32 * u : 32 * (u + 1)]))
+        for lo, hi in ((0, QUARTER), (QUARTER, HALF), (HALF, S)):
+            u, at = divmod(lo, HALF)
+            nc.vector.tensor_copy(x_codes[u][:, at : at + hi - lo], table_words[:].indirect(offsets[:, lo // 16 : hi // 16]))
 
         w1_bf = [keep.tile([P, 2, P * PACK], BF16, name=f"w1_bf{e}", tag=f"w1_bf{e}", align_bytes=64) for e in range(2)]
 
@@ -109,13 +110,13 @@ def tile_picked_inorm_relu_p_kernel(tc, x_words, x_scales, w1, w2, gamma, offs, 
         )
 
         warm_bank = psum.tile([P, HALF], F32, name="warm_bank", tag="bank7")
-        for u in (0, 0, 1, 1):
+        for width in (PIECE, PIECE, PIECE, PIECE, HALF, HALF):
             nc.tensor.matmul_mx(
-                out=warm_bank[0:WARM_COLS, :],
+                out=warm_bank[0:WARM_COLS, 0:width],
                 lhsT=x_codes[0][:, 0:WARM_COLS].bitcast(FP8X4),
                 lhsT_scale=picked_sc[:, 0:WARM_COLS],
-                rhs=x_codes[u][:].bitcast(FP8X4),
-                rhs_scale=picked_sc[:, HALF * u : HALF * (u + 1)],
+                rhs=x_codes[0][:, 0:width].bitcast(FP8X4),
+                rhs_scale=picked_sc[:, 0:width],
                 start=True,
                 stop=True,
             )

@@ -23,7 +23,8 @@ PIECE = 128
 QUARTER = 256
 LAST = 3
 FIRST_COLS = 640
-W1_SPLIT = 80
+EARLY_SPLIT = 80
+LATE_SPLITS = (40, 76)
 COPIED = (0, 2)
 WARM_COLS = 32
 
@@ -38,7 +39,7 @@ def tile_picked_inorm_relu_p_kernel(tc, x_words, x_scales, w1, w2, gamma, offs, 
         offsets = keep.tile([P, S // 16], U16, name="offsets")
         table_words = keep.tile([P, T], U32, name="table_words", align_bytes=64)
         table_scales = reused.tile([P, T], U8, name="table_scales", offset=T)
-        w1_first = keep.tile([P, 2, H], F32, name="w1_first")
+        w1_raw = keep.tile([P, PACK, H], F32, name="w1_raw")
 
         scale_words = table_scales[:].bitcast(I32)
         nc.gpsimd.memset(scale_words[:, :512], 0)
@@ -50,9 +51,8 @@ def tile_picked_inorm_relu_p_kernel(tc, x_words, x_scales, w1, w2, gamma, offs, 
         nc.sync.dma_start(out=table_scales[0:P:8, :].bitcast(I32), in_=x_scales[0].bitcast(I32))
         nc.sync.dma_start(out=table_words[:, FIRST_COLS:].bitcast(I32), in_=words[:, FIRST_COLS:])
         w1_rows = w1.rearrange("(p j) c -> p j c", j=PACK)
-        nc.sync.dma_start(out=w1_first[:], in_=w1_rows[:, :2, :])
-        w1_second = keep.tile([P, 2, H], F32, name="w1_second")
-        nc.sync.dma_start(out=w1_second[:], in_=w1_rows[:, 2:, :])
+        for rows in (slice(0, 2), slice(2, PACK)):
+            nc.sync.dma_start(out=w1_raw[:, rows, :], in_=w1_rows[:, rows, :])
 
         warm_in = keep.tile([P, 1], F32, name="warm_in")
         warm_out = keep.tile([P, 1], F32, name="warm_out")
@@ -73,44 +73,48 @@ def tile_picked_inorm_relu_p_kernel(tc, x_words, x_scales, w1, w2, gamma, offs, 
         nc.vector.tensor_copy(picked_sc[:], table_scales[:].indirect(offsets[:]))
         for r in range(4):
             nc.sync.dma_start(out=x_sc[r:P:32, :].bitcast(I32), in_=picked_sc[8 * r : P : 32, :].bitcast(I32))
-        w1_raw = [w1_first, w1_second]
         gamma_sb = reused.tile([P, PACK], F32, name="gamma_sb", offset=T + 128)
         nc.sync.dma_start(out=gamma_sb[:], in_=gamma.rearrange("(p t) o -> p (t o)", t=PACK))
         w2_raw = reused.tile([P, PACK, N], F32, name="w2_raw", offset=64)
         nc.sync.dma_start(out=w2_raw[:], in_=w2.rearrange("(p j) c -> p j c", j=PACK))
 
         x_codes = [keep.tile([P, HALF], U32, name=f"x_codes{u}", align_bytes=64) for u in range(2)]
-        for lo, hi in ((0, QUARTER), (QUARTER, HALF), (HALF, S)):
+        for lo, hi in ((0, HALF), (HALF, S)):
             u, at = divmod(lo, HALF)
             nc.vector.tensor_copy(x_codes[u][:, at : at + hi - lo], table_words[:].indirect(offsets[:, lo // 16 : hi // 16]))
 
         w1_bf = [keep.tile([P, 2, P * PACK], BF16, name=f"w1_bf{e}", tag=f"w1_bf{e}", align_bytes=64) for e in range(2)]
 
-        def round_w1(engine_copy, a, e, cols=slice(0, P)):
+        def round_w1(engine_copy, rows, e, cols):
             engine_copy(
-                out=w1_bf[e][:].rearrange("p t (m j) -> p m j t", j=PACK)[:, cols, 2 * a : 2 * a + 2, :],
-                in_=w1_raw[a][:].rearrange("p j (m t) -> p m j t", t=PACK)[:, cols, :, 2 * e : 2 * e + 2],
+                out=w1_bf[e][:].rearrange("p t (m j) -> p m j t", j=PACK)[:, cols, rows, :],
+                in_=w1_raw[:].rearrange("p j (m t) -> p m j t", t=PACK)[:, cols, rows, 2 * e : 2 * e + 2],
             )
 
-        round_w1(nc.scalar.copy, 0, 0)
-        round_w1(nc.scalar.copy, 0, 1)
-        round_w1(nc.vector.tensor_copy, 1, 0)
-        round_w1(nc.vector.tensor_copy, 1, 1, slice(0, W1_SPLIT))
-        round_w1(nc.scalar.copy, 1, 1, slice(W1_SPLIT, P))
         w1_codes = keep.tile([P, H], U32, name="w1_codes", align_bytes=64)
         w1_sc = keep.tile([P, H], U8, name="w1_sc", align_bytes=64)
-        for t in (1, 0):
+
+        def quantise_w1(t):
             nc.vector.quantize_mx(
                 out=w1_codes[:, P * t : P * (t + 1)].bitcast(FP8X4), scales=w1_sc[:, P * t : P * (t + 1)],
                 in_=w1_bf[0][:, t, :],
             )
+
+        round_w1(nc.scalar.copy, slice(0, 2), 0, slice(0, P))
+        round_w1(nc.scalar.copy, slice(2, PACK), 0, slice(0, EARLY_SPLIT))
+        round_w1(nc.vector.tensor_copy, slice(2, PACK), 0, slice(EARLY_SPLIT, P))
+        round_w1(nc.vector.tensor_copy, slice(0, PACK), 1, slice(0, LATE_SPLITS[0]))
+        quantise_w1(1)
+        round_w1(nc.vector.tensor_copy, slice(0, PACK), 1, slice(*LATE_SPLITS))
+        quantise_w1(0)
+        round_w1(nc.scalar.copy, slice(0, PACK), 1, slice(LATE_SPLITS[1], P))
         nc.vector.quantize_mx(
             out=w1_codes[:, 2 * P :].bitcast(FP8X4), scales=w1_sc[:, 2 * P :],
             in_=w1_bf[1][:].rearrange("p t c -> p (t c)"),
         )
 
         warm_bank = psum.tile([P, HALF], F32, name="warm_bank", tag="bank7")
-        for width in (PIECE, PIECE, PIECE, PIECE, HALF, HALF):
+        for width in (HALF, HALF, HALF):
             nc.tensor.matmul_mx(
                 out=warm_bank[0:WARM_COLS, 0:width],
                 lhsT=x_codes[0][:, 0:WARM_COLS].bitcast(FP8X4),

@@ -113,17 +113,20 @@ def tile_picked_inorm_relu_p_kernel(tc, x_words, x_scales, w1, w2, gamma, offs, 
             in_=w1_bf[1][:].rearrange("p t c -> p (t c)"),
         )
 
-        warm_bank = psum.tile([P, HALF], F32, name="warm_bank", tag="bank7")
-        for width in (HALF, HALF, HALF):
+        def warm_up(bank):
             nc.tensor.matmul_mx(
-                out=warm_bank[0:WARM_COLS, 0:width],
+                out=bank[0:WARM_COLS, :],
                 lhsT=x_codes[0][:, 0:WARM_COLS].bitcast(FP8X4),
                 lhsT_scale=picked_sc[:, 0:WARM_COLS],
-                rhs=x_codes[0][:, 0:width].bitcast(FP8X4),
-                rhs_scale=picked_sc[:, 0:width],
+                rhs=x_codes[0][:].bitcast(FP8X4),
+                rhs_scale=picked_sc[:, 0:HALF],
                 start=True,
                 stop=True,
             )
+
+        warm_bank = psum.tile([P, HALF], F32, name="warm_bank", tag="bank7")
+        for repeat in range(3):
+            warm_up(warm_bank)
 
         h = {}
         for t, b in [(1, 0), (0, 0), (1, 1), (2, 0), (0, 1), (2, 1), (3, 0), (3, 1)]:
@@ -248,6 +251,8 @@ def tile_picked_inorm_relu_p_kernel(tc, x_words, x_scales, w1, w2, gamma, offs, 
         for t in range(PACK - 1):
             normalise_scalar(t, 1)
         normalise_scalar(3, 1, slice(0, 2 * PIECE))
+
+        warm_up(psum.tile([P, HALF], F32, name="warm_late", tag="bank3"))
 
         pieces = range(S // PIECE)
         z_codes = [keep.tile([P, PIECE], U32, name=f"z_codes{i}", align_bytes=64) for i in pieces]

@@ -22,7 +22,7 @@ HALF = 512
 PIECE = 128
 QUARTER = 256
 LAST = 3
-FIRST_COLS = 640
+FIRST_COLS = 1536
 EARLY_SPLIT = 80
 LATE_SPLITS = (40, 76)
 COPIED = (0, 2)

@@ -23,7 +23,7 @@ PIECE = 128
 QUARTER = 256
 LAST = 3
 FIRST_COLS = 1536
-EARLY_SPLIT = 80
+EARLY_SPLIT = 64
 LATE_SPLITS = (40, 76)
 COPIED = (0, 2)
 WARM_COLS = 32

from contextlib import ExitStack

import concourse.mybir as mybir

K, T, S, H, N = 512, 4096, 1024, 512, 256
FLOPS = 2 * K * H * S + 2 * H * N * S
EPS = 1e-5

F32 = mybir.dt.float32
BF16 = mybir.dt.bfloat16
I32 = mybir.dt.int32
U32 = mybir.dt.uint32
U16 = mybir.dt.uint16
U8 = mybir.dt.uint8
FP8X4 = mybir.dt.float8_e4m3fn_x4
ALU = mybir.AluOpType
ACT = mybir.ActivationFunctionType

P = 128
PACK = 4
HALF = 512
PIECE = 128
QUARTER = 256
LAST = 3
FIRST_COLS = 1536
EARLY_SPLIT = 64
LATE_SPLITS = (40, 76)
COPIED = (0, 2)
WARM_COLS = 32


def tile_picked_inorm_relu_p_kernel(tc, x_words, x_scales, w1, w2, gamma, offs, out):
    nc = tc.nc
    with ExitStack() as ctx:
        keep = ctx.enter_context(tc.tile_pool(name="keep", bufs=1))
        reused = ctx.enter_context(tc.tile_pool(name="reused", bufs=1))
        psum = ctx.enter_context(tc.psum_pool(name="psum", bufs=1))

        offsets = keep.tile([P, S // 16], U16, name="offsets")
        table_words = keep.tile([P, T], U32, name="table_words", align_bytes=64)
        table_scales = reused.tile([P, T], U8, name="table_scales", offset=T)
        w1_raw = keep.tile([P, PACK, H], F32, name="w1_raw")

        scale_words = table_scales[:].bitcast(I32)
        nc.gpsimd.memset(scale_words[:, :512], 0)
        nc.vector.memset(scale_words[:, 512:767], 0)
        nc.vector.memset(scale_words[:, 767:], 0)
        words = x_words[0].rearrange("p n t -> p (n t)").bitcast(I32)
        nc.sync.dma_start(out=table_words[:, :FIRST_COLS].bitcast(I32), in_=words[:, :FIRST_COLS])
        nc.sync.dma_start(offsets[:], offs)
        nc.sync.dma_start(out=table_scales[0:P:8, :].bitcast(I32), in_=x_scales[0].bitcast(I32))
        nc.sync.dma_start(out=table_words[:, FIRST_COLS:].bitcast(I32), in_=words[:, FIRST_COLS:])
        w1_rows = w1.rearrange("(p j) c -> p j c", j=PACK)
        for rows in (slice(0, 2), slice(2, PACK)):
            nc.sync.dma_start(out=w1_raw[:, rows, :], in_=w1_rows[:, rows, :])

        warm_in = keep.tile([P, 1], F32, name="warm_in")
        warm_out = keep.tile([P, 1], F32, name="warm_out")
        nc.gpsimd.memset(warm_in[:], 1.0)
        nc.scalar.activation(out=warm_out[:], in_=warm_in[:], func=ACT.Abs_reciprocal_sqrt)

        stats = [keep.tile([P, 12], F32, name=f"stats{t}") for t in range(PACK)]
        moments = [keep.tile([P, 4], F32, name=f"moments{t}") for t in range(PACK)]
        for t in range(PACK):
            nc.vector.memset(moments[t][:, 1:2], -1.0)
        for t in COPIED:
            nc.vector.memset(moments[t][:, 0:1], -float(HALF))
            nc.vector.memset(stats[t][:, 0:1], float(HALF))

        picked_sc = keep.tile([P, S], U8, name="picked_sc", align_bytes=64)
        x_sc = keep.tile([P, S], U8, name="x_sc", align_bytes=64)
        nc.vector.memset(x_sc[:].bitcast(I32), 0)
        nc.vector.tensor_copy(picked_sc[:], table_scales[:].indirect(offsets[:]))
        for r in range(4):
            nc.sync.dma_start(out=x_sc[r:P:32, :].bitcast(I32), in_=picked_sc[8 * r : P : 32, :].bitcast(I32))
        gamma_sb = reused.tile([P, PACK], F32, name="gamma_sb", offset=T + 128)
        nc.sync.dma_start(out=gamma_sb[:], in_=gamma.rearrange("(p t) o -> p (t o)", t=PACK))
        w2_raw = reused.tile([P, PACK, N], F32, name="w2_raw", offset=64)
        nc.sync.dma_start(out=w2_raw[:], in_=w2.rearrange("(p j) c -> p j c", j=PACK))

        x_codes = [keep.tile([P, HALF], U32, name=f"x_codes{u}", align_bytes=64) for u in range(2)]
        for lo, hi in ((0, HALF), (HALF, S)):
            u, at = divmod(lo, HALF)
            nc.vector.tensor_copy(x_codes[u][:, at : at + hi - lo], table_words[:].indirect(offsets[:, lo // 16 : hi // 16]))

        w1_bf = [keep.tile([P, 2, P * PACK], BF16, name=f"w1_bf{e}", tag=f"w1_bf{e}", align_bytes=64) for e in range(2)]

        def round_w1(engine_copy, rows, e, cols):
            engine_copy(
                out=w1_bf[e][:].rearrange("p t (m j) -> p m j t", j=PACK)[:, cols, rows, :],
                in_=w1_raw[:].rearrange("p j (m t) -> p m j t", t=PACK)[:, cols, rows, 2 * e : 2 * e + 2],
            )

        w1_codes = keep.tile([P, H], U32, name="w1_codes", align_bytes=64)
        w1_sc = keep.tile([P, H], U8, name="w1_sc", align_bytes=64)

        def quantise_w1(t):
            nc.vector.quantize_mx(
                out=w1_codes[:, P * t : P * (t + 1)].bitcast(FP8X4), scales=w1_sc[:, P * t : P * (t + 1)],
                in_=w1_bf[0][:, t, :],
            )

        round_w1(nc.scalar.copy, slice(0, 2), 0, slice(0, P))
        round_w1(nc.scalar.copy, slice(2, PACK), 0, slice(0, EARLY_SPLIT))
        round_w1(nc.vector.tensor_copy, slice(2, PACK), 0, slice(EARLY_SPLIT, P))
        round_w1(nc.vector.tensor_copy, slice(0, PACK), 1, slice(0, LATE_SPLITS[0]))
        quantise_w1(1)
        round_w1(nc.vector.tensor_copy, slice(0, PACK), 1, slice(*LATE_SPLITS))
        quantise_w1(0)
        round_w1(nc.scalar.copy, slice(0, PACK), 1, slice(LATE_SPLITS[1], P))
        nc.vector.quantize_mx(
            out=w1_codes[:, 2 * P :].bitcast(FP8X4), scales=w1_sc[:, 2 * P :],
            in_=w1_bf[1][:].rearrange("p t c -> p (t c)"),
        )

        def warm_up(bank):
            nc.tensor.matmul_mx(
                out=bank[0:WARM_COLS, :],
                lhsT=x_codes[0][:, 0:WARM_COLS].bitcast(FP8X4),
                lhsT_scale=picked_sc[:, 0:WARM_COLS],
                rhs=x_codes[0][:].bitcast(FP8X4),
                rhs_scale=picked_sc[:, 0:HALF],
                start=True,
                stop=True,
            )

        warm_bank = psum.tile([P, HALF], F32, name="warm_bank", tag="bank7")
        for repeat in range(3):
            warm_up(warm_bank)

        h = {}
        for t, b in [(1, 0), (0, 0), (1, 1), (2, 0), (0, 1), (2, 1), (3, 0), (3, 1)]:
            bank = psum.tile([P, HALF], F32, name=f"h{t}{b}", tag=f"bank{2 * t + b}")
            parts = [(b, 0, HALF, 0)] if t < LAST else [(u, QUARTER * b, QUARTER, QUARTER * u) for u in range(2)]
            for u, lo, width, place in parts:
                nc.tensor.matmul_mx(
                    out=bank[:, place : place + width],
                    lhsT=w1_codes[:, P * t : P * (t + 1)].bitcast(FP8X4),
                    lhsT_scale=w1_sc[:, P * t : P * (t + 1)],
                    rhs=x_codes[u][:, lo : lo + width].bitcast(FP8X4),
                    rhs_scale=x_sc[:, HALF * u + lo : HALF * u + lo + width],
                    start=True,
                    stop=True,
                )
            h[t, b] = bank

        def h_of(t, u, cols):
            if t < LAST:
                return h[t, u][:, cols]
            b, lo = divmod(cols.start, QUARTER)
            return h[t, b][:, QUARTER * u + lo : QUARTER * u + lo + cols.stop - cols.start]

        neg_gamma = keep.tile([P, PACK], F32, name="neg_gamma")
        nc.scalar.activation(out=neg_gamma[:], in_=gamma_sb[:], func=ACT.Copy, scale=-1.0)

        z_halves = [keep.tile([P, PACK * HALF], BF16, name=f"z_half{u}", align_bytes=64) for u in range(2)]
        z_rows = [z_half[:].rearrange("p (t n) -> p t n", t=PACK) for z_half in z_halves]
        affine = [keep.tile([P, 3], F32, name=f"affine{t}") for t in range(PACK)]
        rstd = [keep.tile([P, 1], F32, name=f"rstd{t}") for t in range(PACK)]
        shrunk = {t: keep.tile([P, HALF], F32, name=f"shrunk{t}") for t in COPIED}

        def stats_vector(t, u):
            lo = 3 if t in COPIED else 6 * u
            nc.vector.bn_stats(out=stats[t][:, lo : lo + 6], in_=h[t, u][:])

        def sum_scalar(t):
            nc.scalar.activation(
                out=shrunk[t][:], in_=h[t, 0][:], func=ACT.Copy, scale=1.0 / HALF, accum_out=stats[t][:, 1:2]
            )

        def squares_scalar(t):
            squares = keep.tile([P, HALF], BF16, name=f"squares{t}")
            nc.scalar.activation(
                out=squares[:], in_=h[t, 0][:], func=ACT.Square, scale=-1.0, bias=stats[t][:, 1:2],
                accum_out=stats[t][:, 2:3],
            )

        def aggregate(t):
            tuples = stats[t][:, 0:9] if t in COPIED else stats[t][:]
            nc.vector.bn_aggr(out=moments[t][:, 2:4], in_=tuples)

        def root(t):
            nc.scalar.activation(out=rstd[t][:], in_=moments[t][:, 3:4], func=ACT.Abs_reciprocal_sqrt, bias=EPS)

        def affine_vector(t):
            lo = 0 if t in COPIED else 1
            nc.vector.tensor_scalar(
                out=affine[t][:, lo:3], in0=moments[t][:, lo:3], scalar1=neg_gamma[:, t : t + 1], scalar2=rstd[t][:],
                op0=ALU.mult, op1=ALU.mult,
            )

        def affine_scalar(t):
            lo = 0 if t in COPIED else 1
            gained = keep.tile([P, 3 - lo], F32, name=f"gained{t}")
            nc.scalar.activation(out=gained[:], in_=moments[t][:, lo:3], func=ACT.Copy, scale=neg_gamma[:, t : t + 1])
            nc.scalar.activation(out=affine[t][:, lo:3], in_=gained[:], func=ACT.Copy, scale=rstd[t][:])

        def normalise_scalar(t, u, cols=slice(0, HALF)):
            nc.scalar.activation(
                out=z_rows[u][:, t, cols], in_=h_of(t, u, cols), func=ACT.Relu,
                scale=affine[t][:, 1:2], bias=affine[t][:, 2:3],
            )

        def normalise_vector(t, u, cols=slice(0, HALF)):
            source, col = (shrunk[t][:, cols], 0) if t in COPIED and u == 0 else (h_of(t, u, cols), 1)
            nc.vector.tensor_scalar(
                out=z_rows[u][:, t, cols], in0=source, scalar1=affine[t][:, col : col + 1],
                scalar2=affine[t][:, 2:3], op0=ALU.mult, op1=ALU.add,
            )

        w2_bf = keep.tile([P, N, PACK], BF16, name="w2_bf", tag="w1_bf1", align_bytes=64)
        w2_cols = w2_raw[:].rearrange("p j n -> p n j")
        for n0 in range(0, N, P):
            nc.gpsimd.tensor_scalar(
                out=w2_bf[:, n0 : n0 + P, :], in0=w2_cols[:, n0 : n0 + P, :],
                scalar1=1.0, scalar2=0.0, op0=ALU.mult, op1=ALU.add,
            )
        w2_codes = keep.tile([P, N], U32, name="w2_codes", align_bytes=64)
        w2_sc = keep.tile([P, N], U8, name="w2_sc", align_bytes=64)

        sum_scalar(0)
        sum_scalar(2)
        squares_scalar(0)
        stats_vector(1, 0)
        stats_vector(1, 1)
        aggregate(1)
        root(1)
        squares_scalar(2)
        affine_scalar(1)
        stats_vector(0, 1)
        aggregate(0)
        root(0)
        affine_scalar(0)
        stats_vector(2, 1)
        aggregate(2)
        root(2)
        stats_vector(3, 0)
        stats_vector(3, 1)
        aggregate(3)
        root(3)
        normalise_vector(0, 0)
        nc.vector.quantize_mx(out=w2_codes[:].bitcast(FP8X4), scales=w2_sc[:], in_=w2_bf[:].rearrange("p n j -> p (n j)"))
        affine_vector(2)
        affine_vector(3)
        normalise_scalar(1, 0, slice(0, 2 * PIECE))
        normalise_vector(2, 0)
        normalise_vector(3, 0, slice(0, PIECE))
        normalise_vector(3, 0, slice(PIECE, 2 * PIECE))
        normalise_scalar(3, 0, slice(2 * PIECE, HALF))
        normalise_scalar(1, 0, slice(2 * PIECE, HALF))
        for t in range(PACK - 1):
            normalise_scalar(t, 1)
        normalise_scalar(3, 1, slice(0, 2 * PIECE))

        warm_up(psum.tile([P, HALF], F32, name="warm_late", tag="bank3"))

        pieces = range(S // PIECE)
        z_codes = [keep.tile([P, PIECE], U32, name=f"z_codes{i}", align_bytes=64) for i in pieces]
        z_bf = [keep.tile([P, PIECE * PACK], BF16, name=f"z_bf{i}", align_bytes=64) for i in pieces]
        z_sc = [keep.tile([P, PIECE], U8, name=f"z_sc{i}", align_bytes=64) for i in pieces]

        def rows_of(i):
            u, lo = divmod(PIECE * i, HALF)
            return z_rows[u][:, :, lo : lo + PIECE].rearrange("p t (g i) -> p g t i", i=4)

        def words_of(i):
            return z_bf[i][:].rearrange("p (g i t) -> p g t i", i=4, t=PACK)

        def interleave_vector(i):
            nc.vector.tensor_scalar_max(out=words_of(i), in0=rows_of(i), scalar1=0.0)

        def interleave_scalar(i):
            nc.scalar.copy(out=words_of(i), in_=rows_of(i))

        def quantise(i):
            nc.vector.quantize_mx(out=z_codes[i][:].bitcast(FP8X4), scales=z_sc[i][:], in_=z_bf[i][:])

        def product(i, m, acc):
            nc.tensor.matmul_mx(
                out=acc,
                lhsT=w2_codes[:, P * m : P * (m + 1)].bitcast(FP8X4),
                lhsT_scale=w2_sc[:, P * m : P * (m + 1)],
                rhs=z_codes[i][:].bitcast(FP8X4),
                rhs_scale=z_sc[i][:],
                start=True,
                stop=True,
            )

        res = keep.tile([P, 2, S], F32, name="res")

        def second_layer(i, bank, engine_copy):
            acc = psum.tile([P, 2, PIECE], F32, name=f"acc{i}", tag=f"bank{bank}")
            for m in range(2):
                product(i, m, acc[:, m, :])
            engine_copy(out=res[:, :, PIECE * i : PIECE * (i + 1)], in_=acc[:])

        def shared_second_layer(i, banks):
            for m, engine_copy in enumerate((nc.scalar.copy, nc.vector.tensor_copy)):
                acc = psum.tile([P, PIECE], F32, name=f"acc{i}{m}", tag=f"bank{banks[m]}")
                product(i, m, acc[:])
                engine_copy(out=res[:, m, PIECE * i : PIECE * (i + 1)], in_=acc[:])

        def store(first, count):
            cols = slice(PIECE * first, PIECE * (first + count))
            nc.sync.dma_start(out=out.rearrange("(m p) n -> p m n", p=P)[:, :, cols], in_=res[:, :, cols])

        interleave_vector(0)
        interleave_vector(1)
        quantise(0)
        second_layer(0, 0, nc.scalar.copy)
        store(0, 1)
        interleave_vector(2)
        quantise(1)
        second_layer(1, 4, nc.scalar.copy)
        store(1, 1)
        interleave_vector(3)
        quantise(2)
        second_layer(2, 2, nc.scalar.copy)
        normalise_scalar(3, 1, slice(2 * PIECE, HALF))
        interleave_scalar(4)
        interleave_vector(5)
        quantise(3)
        second_layer(3, 6, nc.scalar.copy)
        store(2, 2)
        interleave_vector(6)
        quantise(5)
        second_layer(5, 0, nc.scalar.copy)
        interleave_vector(7)
        quantise(4)
        second_layer(4, 4, nc.scalar.copy)
        store(4, 2)
        quantise(6)
        quantise(7)
        second_layer(6, 1, nc.vector.tensor_copy)
        shared_second_layer(7, (3, 5))
        store(6, 2)
